import numpy as np
import ml_dtypes


def mxq(x, axis, fmt="e4m3"):
    dtype, down = {"e4m3": (ml_dtypes.float8_e4m3fn, 7), "e5m2": (ml_dtypes.float8_e5m2, 14)}[fmt]
    v = np.moveaxis(np.asarray(x, np.float32).astype(ml_dtypes.bfloat16).astype(np.float64), axis, -1)
    blocks = v.reshape(v.shape[:-1] + (-1, 32))
    amax = np.abs(blocks).max(-1, keepdims=True)
    byte = np.maximum(np.where(amax > 0, np.frexp(amax)[1] - 1 + 127, 0) - down, 1)
    scale = np.exp2(byte - 127.0)
    codes = (blocks / scale).astype(np.float32).astype(dtype).astype(np.float64)
    return np.moveaxis((codes * scale).reshape(v.shape), -1, axis)


WIDE = False


def mx_kscale(k):
    if not WIDE:
        return np.ones(k)
    levels = np.array([10, -10, 5, -5, 0])
    if k % 512:
        return np.exp2(np.random.permutation(np.resize(levels, k // 32))).repeat(32)
    a = np.empty((k // 512, 16))
    for p in range(k // 512):
        a[p, :8] = np.random.permutation(np.resize(levels, 8))
        for g in range(8):
            far = levels[np.abs(levels - a[p, g]) >= 10]
            a[p, g + 8] = far[np.random.randint(len(far))]
    return np.exp2(a.ravel()).repeat(32)


def f64(x):
    return np.asarray(x).astype(np.float64)


def striped(idx):
    return np.tile(np.asarray(idx).reshape(-1, 16).T, (8, 1)).astype(np.uint16)


def unstriped(offs):
    return offs[:16].T.reshape(-1).astype(np.int64)


E2M1 = np.array([0.0, 0.5, 1.0, 1.5, 2.0, 3.0, 4.0, 6.0, -0.0, -0.5, -1.0, -1.5, -2.0, -3.0, -4.0, -6.0])


def pack_weight(w, fmt):
    k, n = w.shape
    w = f64(np.asarray(w, np.float32).astype(ml_dtypes.bfloat16)).reshape(k // 32, 32, n)
    amax = np.abs(w).max(1)
    if fmt == "e4m3":
        byte = np.frexp(amax)[1] - 1 + 127 - 7
    else:
        mant, ex = np.frexp(amax / 6.0)
        byte = np.where(mant > 0.5, ex, ex - 1) + 127
    byte = np.clip(np.where(amax > 0, byte, 1), 1, 254)
    scaled = (w * np.exp2(127.0 - byte)[:, None, :]).reshape(k, n).astype(np.float32)
    by_word = np.ascontiguousarray(scaled.reshape(k // 512, 128, 4, n).transpose(0, 1, 3, 2))
    if fmt == "e4m3":
        words = by_word.astype(ml_dtypes.float8_e4m3fn).view(np.uint8)
    else:
        c = by_word.astype(ml_dtypes.float4_e2m1fn).view(np.uint8) & 0xF
        words = (c[..., 0::2] | (c[..., 1::2] << 4)).reshape(k // 512, 128, 2 * n)
    return np.ascontiguousarray(words), np.ascontiguousarray(byte.astype(np.uint8).reshape(k // 512, 16, n))


def unpack_weight(words, scales, fmt):
    g, _, n = scales.shape
    words = np.ascontiguousarray(words).reshape(g, 128, n, -1)
    if fmt == "e4m3":
        vals = words.view(ml_dtypes.float8_e4m3fn).astype(np.float64)
    else:
        nib = np.empty((g, 128, n, 4), np.uint8)
        nib[..., 0::2] = words & 0xF
        nib[..., 1::2] = words >> 4
        vals = E2M1[nib]
    vals = vals * np.repeat(np.exp2(scales.astype(np.float64) - 127.0), 8, axis=1)[..., None]
    return vals.transpose(0, 1, 3, 2).reshape(g * 512, n)


B, N, T, D, DV, NQ = 1, 512, 1024, 1024, 256, 128


def setup_inputs():
    n = np.random.standard_normal
    idx = np.random.permutation(T)[:B * N]
    s = mx_kscale(D)[:, None]
    u = np.ones(T)
    u[idx] = mx_kscale(B * N)
    r = np.random.uniform(0.5, 2.0, T)
    k = n((D, T)) / s
    v = n((DV, T)) / (u * r)
    kp = pack_weight(k, "e2m1")
    return {
        "qT": (n((B, D, NQ)) * s * (0.80 / np.sqrt(D))).astype(np.float32),
        "k_words": np.ascontiguousarray(kp[0].reshape(D // 1024, 2, 128, T, 2).transpose(0, 2, 3, 1, 4)).reshape(D // 1024, 128, T, 4),
        "k_scales": kp[1],
        "vT": v.astype(np.float32),
        "vs": np.tile(u * r, (128, 1)).astype(np.float32),
        "og": n((B, NQ, DV)).astype(np.float32),
        "offs": striped(idx),
    }


def reference(qT, k_words, k_scales, vT, vs, og, offs):
    idx = unstriped(offs)
    k = unpack_weight(k_words.reshape(D // 1024, 128, T, 2, 2).transpose(0, 3, 1, 2, 4).reshape(D // 512, 128, 2 * T), k_scales, "e2m1")
    v = f64(vT)
    pick = lambda x: x[:, idx].reshape(x.shape[0], B, N).transpose(1, 0, 2)
    q = f64(qT)
    score = mxq(q, 1, "e4m3").transpose(0, 2, 1) @ pick(k)
    m = score.max(-1, keepdims=True)
    p = np.exp(score - m)
    total = p.sum(-1, keepdims=True)
    w = p * pick(f64(vs))[:, :1, :]
    y = mxq(w, 2, "e4m3") @ mxq(pick(v).transpose(0, 2, 1), 1, "e4m3")
    y = y / total
    y = y / (1.0 + np.exp(-f64(og)))
    return y

@@ -1,0 +1,143 @@
+from contextlib import ExitStack
+
+import concourse.mybir as mybir
+from concourse.masks import make_identity
+
+T, N, D, DV, NQ = 1024, 512, 1024, 256, 128
+P = 128
+PACK = 4
+PASSES = D // (P * PACK)
+
+FLOPS = 2 * NQ * N * (D + DV)
+
+F32 = mybir.dt.float32
+BF16 = mybir.dt.bfloat16
+I32 = mybir.dt.int32
+U32 = mybir.dt.uint32
+U16 = mybir.dt.uint16
+U8 = mybir.dt.uint8
+FP8X4 = mybir.dt.float8_e4m3fn_x4
+FP4X4 = mybir.dt.float4_e2m1fn_x4
+ACT = mybir.ActivationFunctionType
+ALU = mybir.AluOpType
+AXIS = mybir.AxisListType
+
+V_CHUNKS = ((0, 512), (512, 768), (768, 1024))
+
+
+def tile_attend_gate_topk_kernel(tc, qT, k_words, k_scales, vT, vs, og, offs, out):
+    nc = tc.nc
+    with ExitStack() as ctx:
+        sb = ctx.enter_context(tc.tile_pool(name="sb", bufs=1))
+        ps = ctx.enter_context(tc.psum_pool(name="ps", bufs=1))
+
+        offsets = sb.tile([P, N // 16], U16, name="offsets")
+        vs_pool = sb.tile([P, T], F32, name="vs_pool")
+        kw_pool = sb.tile([P, T], I32, name="kw_pool")
+        ks_pool = sb.tile([P, PASSES, T], U8, name="ks_pool", align_bytes=64)
+        gate_in = sb.tile([P, DV], F32, name="gate_in")
+        q_raw = sb.tile([P, PASSES, PACK, NQ], F32, name="q_raw")
+        v_raw = [sb.tile([P, 2, b - a], F32, name="v_raw%d" % a) for a, b in V_CHUNKS]
+        ident = sb.tile([P, P], F32, name="ident")
+
+        nc.sync.dma_start(offsets[:], offs)
+        nc.sync.dma_start(out=vs_pool[P - 1:P, :], in_=vs[0:1, :])
+        nc.scalar.dma_start(out=gate_in[:], in_=og[0])
+        ks_words = ks_pool[:].rearrange("p o t -> p (o t)").bitcast(I32)
+        nc.vector.memset(vs_pool[0:P - 1, :], 0.0)
+        nc.vector.memset(ks_words, 0)
+        nc.sync.dma_start(out=kw_pool[:], in_=k_words[0].rearrange("p t b -> p (t b)").bitcast(I32))
+        nc.sync.dma_start(out=q_raw[:], in_=qT[0].rearrange("(o p j) q -> p o j q", o=PASSES, j=PACK))
+        ks_rows = k_scales.bitcast(I32).rearrange("o (quad r) w -> r quad o w", r=4)
+        ks_dst = ks_words.rearrange("p (o w) -> p o w", o=PASSES)
+        for r in range(4):
+            nc.sync.dma_start(out=ks_dst[r:P:32, :, :], in_=ks_rows[r])
+        v_rows = vT.rearrange("(c h) t -> c h t", h=2)
+        for i, (a, b) in enumerate(V_CHUNKS):
+            nc.sync.dma_start(out=v_raw[i][:], in_=v_rows[:, :, a:b])
+        make_identity(nc, ident[:])
+
+        th = sb.tile([P, DV], F32, name="th")
+        nc.scalar.activation(out=th[:], in_=gate_in[:], func=ACT.Tanh, scale=0.5)
+
+        vs_g = sb.tile([P, N], F32, name="vs_g")
+        nc.vector.tensor_copy(out=vs_g[:], in_=vs_pool[:].indirect(offsets[:]))
+
+        kw_g = sb.tile([P, N], U32, name="kw_g")
+        nc.vector.tensor_copy(out=kw_g[:], in_=kw_pool[:].bitcast(U32).indirect(offsets[:]))
+        ks_g = [sb.tile([P, N], U8, name="ks_g%d" % o, align_bytes=64) for o in range(PASSES)]
+        k_op = sb.tile([P, PASSES, N], U16, name="k_op", align_bytes=64)
+        nc.vector.tensor_copy(out=ks_g[0][:], in_=ks_pool[:, 0, :].indirect(offsets[:]))
+        nc.vector.tensor_copy(out=k_op[:], in_=kw_g[:].bitcast(U16).rearrange("p (n o) -> p o n", o=PASSES))
+
+        q_il = sb.tile([P, PASSES, NQ, PACK], BF16, name="q_il", align_bytes=64)
+        nc.scalar.copy(out=q_il[:], in_=q_raw[:].rearrange("p o j q -> p o q j"))
+        q_codes = sb.tile([P, PASSES * NQ], U32, name="q_codes", align_bytes=64)
+        q_sc = sb.tile([P, PASSES * NQ], U8, name="q_sc", align_bytes=64)
+        nc.vector.quantize_mx(out=q_codes[:].bitcast(FP8X4), scales=q_sc[:],
+                              in_=q_il[:].rearrange("p o q j -> p (o q j)"))
+        nc.vector.tensor_copy(out=ks_g[1][:], in_=ks_pool[:, 1, :].indirect(offsets[:]))
+
+        scores = ps.tile([P, N], F32, name="scores")
+        for o in range(PASSES):
+            cols = slice(o * NQ, (o + 1) * NQ)
+            nc.tensor.matmul_mx(out=scores[:], lhsT=q_codes[:, cols].bitcast(FP8X4), lhsT_scale=q_sc[:, cols],
+                                rhs=k_op[:, o, :].bitcast(FP4X4), rhs_scale=ks_g[o][:],
+                                start=(o == 0), stop=(o == PASSES - 1))
+
+        vs_ps = ps.tile([P, PACK, P], F32, name="vs_ps")
+        for t in range(PACK):
+            nc.tensor.transpose(vs_ps[:, t, :], vs_g[:, t:N:PACK], ident[:])
+        vs_col = sb.tile([P, PACK], F32, name="vs_col")
+        nc.scalar.copy(out=vs_col[:], in_=vs_ps[:, :, P - 1])
+
+        v_pool = sb.tile([P, T, 2], BF16, name="v_pool", align_bytes=64)
+        for i, (a, b) in enumerate(V_CHUNKS):
+            nc.scalar.activation(out=v_pool[:, a:b, :], in_=v_raw[i][:].rearrange("c h t -> c t h"), func=ACT.Copy)
+        v_g = sb.tile([P, N], U32, name="v_g")
+        v_window = v_pool[:].rearrange("c t h -> c (t h)").bitcast(U32)
+        nc.vector.tensor_copy(out=v_g[:], in_=v_window.indirect(offsets[:]))
+
+        neg_m = sb.tile([P, 1], F32, name="neg_m")
+        nc.vector.tensor_reduce(out=neg_m[:], in_=scores[:], axis=AXIS.X, op=ALU.max, negate=True)
+        p_sb = sb.tile([P, PACK, P], F32, name="p_sb")
+        l_half = [sb.tile([P, 1], F32, name="l_half%d" % u) for u in range(2)]
+        s_by_t = scores[:].rearrange("q (s t) -> q t s", t=PACK)
+        p_ps = ps.tile([P, PACK, NQ], F32, name="p_ps")
+        v_ps = ps.tile([P, PACK, P], F32, name="v_ps")
+        v_g_words = v_g[:].bitcast(F32)
+        for t in range(PACK):
+            nc.tensor.transpose(v_ps[:, t, :], v_g_words[:, t:N:PACK], ident[:])
+        for u in range(2):
+            nc.scalar.activation(out=p_sb[:, 2 * u:2 * u + 2, :], in_=s_by_t[:, 2 * u:2 * u + 2, :], func=ACT.Exp,
+                                 bias=neg_m[:], scale=1.0, accum_out=l_half[u][:])
+            for t in (2 * u, 2 * u + 1):
+                nc.tensor.transpose(p_ps[:, t, :], p_sb[:, t, :], ident[:])
+        v_il = sb.tile([P, DV, PACK], BF16, name="v_il", align_bytes=64)
+        v_ps_bf = v_ps[:].rearrange("s t c -> s (t c)").bitcast(BF16)
+        nc.scalar.copy(out=v_il[:], in_=v_ps_bf.rearrange("s (t e) -> s e t", t=PACK))
+
+        l_sum = sb.tile([P, 1], F32, name="l_sum")
+        nc.vector.tensor_tensor(out=l_sum[:], in0=l_half[0][:], in1=l_half[1][:], op=ALU.add)
+        w_il = sb.tile([P, NQ, PACK], BF16, name="w_il", align_bytes=64)
+        nc.vector.tensor_tensor(out=w_il[:], in0=p_ps[:].rearrange("s t q -> s q t"),
+                                in1=vs_col[:].unsqueeze(1).to_broadcast([P, NQ, PACK]), op=ALU.mult)
+        r_sum = sb.tile([P, 1], F32, name="r_sum")
+        nc.vector.reciprocal(out=r_sum[:], in_=l_sum[:])
+        v_codes = sb.tile([P, DV], U32, name="v_codes", align_bytes=64)
+        v_sc = sb.tile([P, DV], U8, name="v_sc", align_bytes=64)
+        nc.vector.quantize_mx(out=v_codes[:].bitcast(FP8X4), scales=v_sc[:],
+                              in_=v_il[:].rearrange("s e t -> s (e t)"))
+        w_codes = sb.tile([P, NQ], U32, name="w_codes", align_bytes=64)
+        w_sc = sb.tile([P, NQ], U8, name="w_sc", align_bytes=64)
+        nc.vector.quantize_mx(out=w_codes[:].bitcast(FP8X4), scales=w_sc[:],
+                              in_=w_il[:].rearrange("s q t -> s (q t)"))
+        y_ps = ps.tile([P, DV], F32, name="y_ps")
+        nc.tensor.matmul_mx(out=y_ps[:], lhsT=w_codes[:].bitcast(FP8X4), lhsT_scale=w_sc[:],
+                            rhs=v_codes[:].bitcast(FP8X4), rhs_scale=v_sc[:], start=True, stop=True)
+
+        gate = sb.tile([P, DV], F32, name="gate")
+        nc.scalar.activation(out=gate[:], in_=th[:], func=ACT.Identity, bias=r_sum[:], scale=r_sum[:])
+        res = sb.tile([P, DV], F32, name="res")
+        nc.vector.scalar_tensor_tensor(out=res[:], in0=y_ps[:], scalar=0.5, in1=gate[:], op0=ALU.mult, op1=ALU.mult)
+        nc.sync.dma_start(out=out[0], in_=res[:])

@@ -22,7 +22,7 @@ ACT = mybir.ActivationFunctionType
 ALU = mybir.AluOpType
 AXIS = mybir.AxisListType
 
-V_CHUNKS = ((0, 512), (512, 768), (768, 1024))
+V_CHUNKS = ((0, 256), (256, 512), (512, 768), (768, 1024))
 
 
 def tile_attend_gate_topk_kernel(tc, qT, k_words, k_scales, vT, vs, og, offs, out):
@@ -35,87 +35,92 @@ def tile_attend_gate_topk_kernel(tc, qT, k_words, k_scales, vT, vs, og, offs, ou
         vs_pool = sb.tile([P, T], F32, name="vs_pool")
         kw_pool = sb.tile([P, T], I32, name="kw_pool")
         ks_pool = sb.tile([P, PASSES, T], U8, name="ks_pool", align_bytes=64)
-        gate_in = sb.tile([P, DV], F32, name="gate_in")
-        q_raw = sb.tile([P, PASSES, PACK, NQ], F32, name="q_raw")
+        q_raw = [sb.tile([P, PACK, NQ], F32, name="q_raw%d" % o) for o in range(PASSES)]
         v_raw = [sb.tile([P, 2, b - a], F32, name="v_raw%d" % a) for a, b in V_CHUNKS]
+        gate_in = sb.tile([P, DV], F32, name="gate_in")
         ident = sb.tile([P, P], F32, name="ident")
 
         nc.sync.dma_start(offsets[:], offs)
         nc.sync.dma_start(out=vs_pool[P - 1:P, :], in_=vs[0:1, :])
-        nc.scalar.dma_start(out=gate_in[:], in_=og[0])
-        ks_words = ks_pool[:].rearrange("p o t -> p (o t)").bitcast(I32)
-        nc.vector.memset(vs_pool[0:P - 1, :], 0.0)
-        nc.vector.memset(ks_words, 0)
         nc.sync.dma_start(out=kw_pool[:], in_=k_words[0].rearrange("p t b -> p (t b)").bitcast(I32))
-        nc.sync.dma_start(out=q_raw[:], in_=qT[0].rearrange("(o p j) q -> p o j q", o=PASSES, j=PACK))
+        ks_words = ks_pool[:].rearrange("p o t -> p (o t)").bitcast(I32)
+        nc.vector.memset(ks_words, 0)
+        nc.vector.memset(vs_pool[0:P - 1, :], 0.0)
         ks_rows = k_scales.bitcast(I32).rearrange("o (quad r) w -> r quad o w", r=4)
         ks_dst = ks_words.rearrange("p (o w) -> p o w", o=PASSES)
         for r in range(4):
             nc.sync.dma_start(out=ks_dst[r:P:32, :, :], in_=ks_rows[r])
+        rows = qT[0].rearrange("(o p j) q -> o p j q", o=PASSES, j=PACK)
+        for o in range(PASSES):
+            nc.sync.dma_start(out=q_raw[o][:], in_=rows[o])
         v_rows = vT.rearrange("(c h) t -> c h t", h=2)
         for i, (a, b) in enumerate(V_CHUNKS):
             nc.sync.dma_start(out=v_raw[i][:], in_=v_rows[:, :, a:b])
+        nc.sync.dma_start(out=gate_in[:], in_=og[0])
         make_identity(nc, ident[:])
-
-        th = sb.tile([P, DV], F32, name="th")
-        nc.scalar.activation(out=th[:], in_=gate_in[:], func=ACT.Tanh, scale=0.5)
 
         vs_g = sb.tile([P, N], F32, name="vs_g")
         nc.vector.tensor_copy(out=vs_g[:], in_=vs_pool[:].indirect(offsets[:]))
+        vs_ps = ps.tile([P, PACK, P], F32, name="vs_ps")
+        for t in range(PACK):
+            nc.tensor.transpose(vs_ps[:, t, :], vs_g[:, t:N:PACK], ident[:])
 
         kw_g = sb.tile([P, N], U32, name="kw_g")
         nc.vector.tensor_copy(out=kw_g[:], in_=kw_pool[:].bitcast(U32).indirect(offsets[:]))
         ks_g = [sb.tile([P, N], U8, name="ks_g%d" % o, align_bytes=64) for o in range(PASSES)]
-        k_op = sb.tile([P, PASSES, N], U16, name="k_op", align_bytes=64)
         nc.vector.tensor_copy(out=ks_g[0][:], in_=ks_pool[:, 0, :].indirect(offsets[:]))
-        nc.vector.tensor_copy(out=k_op[:], in_=kw_g[:].bitcast(U16).rearrange("p (n o) -> p o n", o=PASSES))
 
         q_il = sb.tile([P, PASSES, NQ, PACK], BF16, name="q_il", align_bytes=64)
-        nc.scalar.copy(out=q_il[:], in_=q_raw[:].rearrange("p o j q -> p o q j"))
+        for o in range(PASSES):
+            nc.scalar.activation(out=q_il[:, o, :, :], in_=q_raw[o][:].rearrange("p j q -> p q j"), func=ACT.Copy)
         q_codes = sb.tile([P, PASSES * NQ], U32, name="q_codes", align_bytes=64)
         q_sc = sb.tile([P, PASSES * NQ], U8, name="q_sc", align_bytes=64)
-        nc.vector.quantize_mx(out=q_codes[:].bitcast(FP8X4), scales=q_sc[:],
-                              in_=q_il[:].rearrange("p o q j -> p (o q j)"))
+        k_op = sb.tile([P, PASSES, N], U16, name="k_op", align_bytes=64)
+        kw_halves = kw_g[:].bitcast(U16).rearrange("p (n o) -> p o n", o=PASSES)
+
+        def quantise_queries(o):
+            cols = slice(o * NQ, (o + 1) * NQ)
+            nc.vector.quantize_mx(out=q_codes[:, cols].bitcast(FP8X4), scales=q_sc[:, cols],
+                                  in_=q_il[:, o, :, :].rearrange("p q j -> p (q j)"))
+
+        quantise_queries(0)
+        for o in range(PASSES):
+            nc.vector.tensor_copy(out=k_op[:, o, :], in_=kw_halves[:, o, :])
+        quantise_queries(1)
         nc.vector.tensor_copy(out=ks_g[1][:], in_=ks_pool[:, 1, :].indirect(offsets[:]))
 
         scores = ps.tile([P, N], F32, name="scores")
-        for o in range(PASSES):
+        for o, plane in enumerate(ks_g):
             cols = slice(o * NQ, (o + 1) * NQ)
             nc.tensor.matmul_mx(out=scores[:], lhsT=q_codes[:, cols].bitcast(FP8X4), lhsT_scale=q_sc[:, cols],
-                                rhs=k_op[:, o, :].bitcast(FP4X4), rhs_scale=ks_g[o][:],
+                                rhs=k_op[:, o, :].bitcast(FP4X4), rhs_scale=plane[:],
                                 start=(o == 0), stop=(o == PASSES - 1))
 
-        vs_ps = ps.tile([P, PACK, P], F32, name="vs_ps")
-        for t in range(PACK):
-            nc.tensor.transpose(vs_ps[:, t, :], vs_g[:, t:N:PACK], ident[:])
         vs_col = sb.tile([P, PACK], F32, name="vs_col")
-        nc.scalar.copy(out=vs_col[:], in_=vs_ps[:, :, P - 1])
+        nc.scalar.activation(out=vs_col[:], in_=vs_ps[:, :, P - 1], func=ACT.Copy)
 
-        v_pool = sb.tile([P, T, 2], BF16, name="v_pool", align_bytes=64)
+        v_pool = sb.tile([P, T, 2], BF16, name="v_pool", tag="v_chain", align_bytes=64)
         for i, (a, b) in enumerate(V_CHUNKS):
             nc.scalar.activation(out=v_pool[:, a:b, :], in_=v_raw[i][:].rearrange("c h t -> c t h"), func=ACT.Copy)
-        v_g = sb.tile([P, N], U32, name="v_g")
-        v_window = v_pool[:].rearrange("c t h -> c (t h)").bitcast(U32)
-        nc.vector.tensor_copy(out=v_g[:], in_=v_window.indirect(offsets[:]))
 
-        neg_m = sb.tile([P, 1], F32, name="neg_m")
+        v_g = sb.tile([P, PACK, P], U32, name="v_g", align_bytes=64)
+        v_window = v_pool[:].rearrange("c t h -> c (t h)").bitcast(U32)
+        nc.vector.tensor_copy(out=v_g[:].rearrange("c t s -> c s t"), in_=v_window.indirect(offsets[:]))
+        v_ps = ps.tile([P, PACK, P], F32, name="v_ps")
+        for t in range(PACK):
+            nc.tensor.transpose(v_ps[:, t, :], v_g[:, t, :].bitcast(F32), ident[:])
+
+        neg_m = sb.tile([P, 1], F32, name="neg_m", tag="v_chain", align_bytes=64)
         nc.vector.tensor_reduce(out=neg_m[:], in_=scores[:], axis=AXIS.X, op=ALU.max, negate=True)
         p_sb = sb.tile([P, PACK, P], F32, name="p_sb")
         l_half = [sb.tile([P, 1], F32, name="l_half%d" % u) for u in range(2)]
         s_by_t = scores[:].rearrange("q (s t) -> q t s", t=PACK)
         p_ps = ps.tile([P, PACK, NQ], F32, name="p_ps")
-        v_ps = ps.tile([P, PACK, P], F32, name="v_ps")
-        v_g_words = v_g[:].bitcast(F32)
-        for t in range(PACK):
-            nc.tensor.transpose(v_ps[:, t, :], v_g_words[:, t:N:PACK], ident[:])
         for u in range(2):
             nc.scalar.activation(out=p_sb[:, 2 * u:2 * u + 2, :], in_=s_by_t[:, 2 * u:2 * u + 2, :], func=ACT.Exp,
                                  bias=neg_m[:], scale=1.0, accum_out=l_half[u][:])
             for t in (2 * u, 2 * u + 1):
                 nc.tensor.transpose(p_ps[:, t, :], p_sb[:, t, :], ident[:])
-        v_il = sb.tile([P, DV, PACK], BF16, name="v_il", align_bytes=64)
-        v_ps_bf = v_ps[:].rearrange("s t c -> s (t c)").bitcast(BF16)
-        nc.scalar.copy(out=v_il[:], in_=v_ps_bf.rearrange("s (t e) -> s e t", t=PACK))
 
         l_sum = sb.tile([P, 1], F32, name="l_sum")
         nc.vector.tensor_tensor(out=l_sum[:], in0=l_half[0][:], in1=l_half[1][:], op=ALU.add)
@@ -124,20 +129,31 @@ def tile_attend_gate_topk_kernel(tc, qT, k_words, k_scales, vT, vs, og, offs, ou
                                 in1=vs_col[:].unsqueeze(1).to_broadcast([P, NQ, PACK]), op=ALU.mult)
         r_sum = sb.tile([P, 1], F32, name="r_sum")
         nc.vector.reciprocal(out=r_sum[:], in_=l_sum[:])
-        v_codes = sb.tile([P, DV], U32, name="v_codes", align_bytes=64)
-        v_sc = sb.tile([P, DV], U8, name="v_sc", align_bytes=64)
-        nc.vector.quantize_mx(out=v_codes[:].bitcast(FP8X4), scales=v_sc[:],
-                              in_=v_il[:].rearrange("s e t -> s (e t)"))
         w_codes = sb.tile([P, NQ], U32, name="w_codes", align_bytes=64)
         w_sc = sb.tile([P, NQ], U8, name="w_sc", align_bytes=64)
         nc.vector.quantize_mx(out=w_codes[:].bitcast(FP8X4), scales=w_sc[:],
                               in_=w_il[:].rearrange("s q t -> s (q t)"))
-        y_ps = ps.tile([P, DV], F32, name="y_ps")
-        nc.tensor.matmul_mx(out=y_ps[:], lhsT=w_codes[:].bitcast(FP8X4), lhsT_scale=w_sc[:],
-                            rhs=v_codes[:].bitcast(FP8X4), rhs_scale=v_sc[:], start=True, stop=True)
 
+        th = sb.tile([P, DV], F32, name="th")
+        nc.scalar.activation(out=th[:], in_=gate_in[:], func=ACT.Tanh, scale=0.5)
+        v_il = sb.tile([P, DV, PACK], BF16, name="v_il", tag="v_chain", align_bytes=64)
+        v_ps_bf = v_ps[:].rearrange("s t c -> s (t c)").bitcast(BF16).rearrange("s (t e) -> s e t", t=PACK)
+        v_codes = sb.tile([P, DV], U32, name="v_codes", align_bytes=64)
+        v_sc = sb.tile([P, DV], U8, name="v_sc", align_bytes=64)
+        half = DV // 2
+        for u in range(2):
+            cols = slice(u * half, (u + 1) * half)
+            nc.scalar.copy(out=v_il[:, cols, :], in_=v_ps_bf[:, cols, :])
+            nc.vector.quantize_mx(out=v_codes[:, cols].bitcast(FP8X4), scales=v_sc[:, cols],
+                                  in_=v_il[:, cols, :].rearrange("s e t -> s (e t)"))
         gate = sb.tile([P, DV], F32, name="gate")
         nc.scalar.activation(out=gate[:], in_=th[:], func=ACT.Identity, bias=r_sum[:], scale=r_sum[:])
-        res = sb.tile([P, DV], F32, name="res")
-        nc.vector.scalar_tensor_tensor(out=res[:], in0=y_ps[:], scalar=0.5, in1=gate[:], op0=ALU.mult, op1=ALU.mult)
-        nc.sync.dma_start(out=out[0], in_=res[:])
+        for u, queue in enumerate((nc.sync, nc.scalar)):
+            cols = slice(u * half, (u + 1) * half)
+            y_ps = ps.tile([P, half], F32, name="y_ps%d" % u)
+            nc.tensor.matmul_mx(out=y_ps[:], lhsT=w_codes[:].bitcast(FP8X4), lhsT_scale=w_sc[:],
+                                rhs=v_codes[:, cols].bitcast(FP8X4), rhs_scale=v_sc[:, cols], start=True, stop=True)
+            res = sb.tile([P, half], F32, name="res%d" % u)
+            nc.vector.scalar_tensor_tensor(out=res[:], in0=y_ps[:], scalar=0.5, in1=gate[:, cols],
+                                           op0=ALU.mult, op1=ALU.mult)
+            queue.dma_start(out=out[0, :, cols], in_=res[:])

@@ -7,6 +7,10 @@ T, N, D, DV, NQ = 1024, 512, 1024, 256, 128
 P = 128
 PACK = 4
 PASSES = D // (P * PACK)
+SCALE_ROWS = 4
+SECOND = 16
+V_CHUNK = 256
+HALF = DV // 2
 
 FLOPS = 2 * NQ * N * (D + DV)
 
@@ -22,8 +26,6 @@ ACT = mybir.ActivationFunctionType
 ALU = mybir.AluOpType
 AXIS = mybir.AxisListType
 
-V_CHUNKS = ((0, 256), (256, 512), (512, 768), (768, 1024))
-
 
 def tile_attend_gate_topk_kernel(tc, qT, k_words, k_scales, vT, vs, og, offs, out):
     nc = tc.nc
@@ -34,28 +36,29 @@ def tile_attend_gate_topk_kernel(tc, qT, k_words, k_scales, vT, vs, og, offs, ou
         offsets = sb.tile([P, N // 16], U16, name="offsets")
         vs_pool = sb.tile([P, T], F32, name="vs_pool")
         kw_pool = sb.tile([P, T], I32, name="kw_pool")
-        ks_pool = sb.tile([P, PASSES, T], U8, name="ks_pool", align_bytes=64)
+        ks_pool = sb.tile([P, T], U8, name="ks_pool", tag="scales_then_words", align_bytes=64)
+        ks_second = sb.tile([P, N], U8, name="ks_second", align_bytes=64)
         q_raw = [sb.tile([P, PACK, NQ], F32, name="q_raw%d" % o) for o in range(PASSES)]
-        v_raw = [sb.tile([P, 2, b - a], F32, name="v_raw%d" % a) for a, b in V_CHUNKS]
+        v_raw = [sb.tile([P, 2, V_CHUNK], F32, name="v_raw%d" % i) for i in range(T // V_CHUNK)]
         gate_in = sb.tile([P, DV], F32, name="gate_in")
         ident = sb.tile([P, P], F32, name="ident")
 
         nc.sync.dma_start(offsets[:], offs)
         nc.sync.dma_start(out=vs_pool[P - 1:P, :], in_=vs[0:1, :])
         nc.sync.dma_start(out=kw_pool[:], in_=k_words[0].rearrange("p t b -> p (t b)").bitcast(I32))
-        ks_words = ks_pool[:].rearrange("p o t -> p (o t)").bitcast(I32)
+        ks_words = ks_pool[:].bitcast(I32)
         nc.vector.memset(ks_words, 0)
         nc.vector.memset(vs_pool[0:P - 1, :], 0.0)
-        ks_rows = k_scales.bitcast(I32).rearrange("o (quad r) w -> r quad o w", r=4)
-        ks_dst = ks_words.rearrange("p (o w) -> p o w", o=PASSES)
-        for r in range(4):
-            nc.sync.dma_start(out=ks_dst[r:P:32, :, :], in_=ks_rows[r])
-        rows = qT[0].rearrange("(o p j) q -> o p j q", o=PASSES, j=PACK)
+        nc.vector.memset(ks_second[:].bitcast(I32), 0)
+        ks_rows = k_scales.bitcast(I32).rearrange("o (quad r) w -> r quad o w", r=SCALE_ROWS)
+        for r in range(SCALE_ROWS):
+            nc.sync.dma_start(out=ks_words[r:P:SECOND, :], in_=ks_rows[r])
+        q_rows = qT[0].rearrange("(o p j) q -> o p j q", o=PASSES, j=PACK)
         for o in range(PASSES):
-            nc.sync.dma_start(out=q_raw[o][:], in_=rows[o])
+            nc.sync.dma_start(out=q_raw[o][:], in_=q_rows[o])
         v_rows = vT.rearrange("(c h) t -> c h t", h=2)
-        for i, (a, b) in enumerate(V_CHUNKS):
-            nc.sync.dma_start(out=v_raw[i][:], in_=v_rows[:, :, a:b])
+        for i in range(T // V_CHUNK):
+            nc.sync.dma_start(out=v_raw[i][:], in_=v_rows[:, :, i * V_CHUNK:(i + 1) * V_CHUNK])
         nc.sync.dma_start(out=gate_in[:], in_=og[0])
         make_identity(nc, ident[:])
 
@@ -65,14 +68,15 @@ def tile_attend_gate_topk_kernel(tc, qT, k_words, k_scales, vT, vs, og, offs, ou
         for t in range(PACK):
             nc.tensor.transpose(vs_ps[:, t, :], vs_g[:, t:N:PACK], ident[:])
 
-        kw_g = sb.tile([P, N], U32, name="kw_g")
+        ks_g = sb.tile([P, N], U8, name="ks_g", align_bytes=64)
+        nc.vector.tensor_copy(out=ks_g[:], in_=ks_pool[:].indirect(offsets[:]))
+        nc.sync.dma_start(out=ks_second[:].bitcast(I32)[0:P - SECOND, :], in_=ks_g[:].bitcast(I32)[SECOND:P, :])
+        kw_g = sb.tile([P, N], U32, name="kw_g", tag="scales_then_words", align_bytes=64)
         nc.vector.tensor_copy(out=kw_g[:], in_=kw_pool[:].bitcast(U32).indirect(offsets[:]))
-        ks_g = [sb.tile([P, N], U8, name="ks_g%d" % o, align_bytes=64) for o in range(PASSES)]
-        nc.vector.tensor_copy(out=ks_g[0][:], in_=ks_pool[:, 0, :].indirect(offsets[:]))
 
         q_il = sb.tile([P, PASSES, NQ, PACK], BF16, name="q_il", align_bytes=64)
-        for o in range(PASSES):
-            nc.scalar.activation(out=q_il[:, o, :, :], in_=q_raw[o][:].rearrange("p j q -> p q j"), func=ACT.Copy)
+        q_by_query = [q_raw[o][:].rearrange("p j q -> p q j") for o in range(PASSES)]
+        nc.scalar.activation(out=q_il[:, 0, :, :], in_=q_by_query[0], func=ACT.Copy)
         q_codes = sb.tile([P, PASSES * NQ], U32, name="q_codes", align_bytes=64)
         q_sc = sb.tile([P, PASSES * NQ], U8, name="q_sc", align_bytes=64)
         k_op = sb.tile([P, PASSES, N], U16, name="k_op", align_bytes=64)
@@ -84,13 +88,13 @@ def tile_attend_gate_topk_kernel(tc, qT, k_words, k_scales, vT, vs, og, offs, ou
                                   in_=q_il[:, o, :, :].rearrange("p q j -> p (q j)"))
 
         quantise_queries(0)
+        nc.vector.tensor_copy(out=q_il[:, 1, :, :], in_=q_by_query[1])
         for o in range(PASSES):
             nc.vector.tensor_copy(out=k_op[:, o, :], in_=kw_halves[:, o, :])
         quantise_queries(1)
-        nc.vector.tensor_copy(out=ks_g[1][:], in_=ks_pool[:, 1, :].indirect(offsets[:]))
 
         scores = ps.tile([P, N], F32, name="scores")
-        for o, plane in enumerate(ks_g):
+        for o, plane in enumerate((ks_g, ks_second)):
             cols = slice(o * NQ, (o + 1) * NQ)
             nc.tensor.matmul_mx(out=scores[:], lhsT=q_codes[:, cols].bitcast(FP8X4), lhsT_scale=q_sc[:, cols],
                                 rhs=k_op[:, o, :].bitcast(FP4X4), rhs_scale=plane[:],
@@ -100,8 +104,8 @@ def tile_attend_gate_topk_kernel(tc, qT, k_words, k_scales, vT, vs, og, offs, ou
         nc.scalar.activation(out=vs_col[:], in_=vs_ps[:, :, P - 1], func=ACT.Copy)
 
         v_pool = sb.tile([P, T, 2], BF16, name="v_pool", tag="v_chain", align_bytes=64)
-        for i, (a, b) in enumerate(V_CHUNKS):
-            nc.scalar.activation(out=v_pool[:, a:b, :], in_=v_raw[i][:].rearrange("c h t -> c t h"), func=ACT.Copy)
+        for i in range(T // V_CHUNK):
+            nc.scalar.activation(out=v_pool[:, i * V_CHUNK:(i + 1) * V_CHUNK, :], in_=v_raw[i][:].rearrange("c h t -> c t h"), func=ACT.Copy)
 
         v_g = sb.tile([P, PACK, P], U32, name="v_g", align_bytes=64)
         v_window = v_pool[:].rearrange("c t h -> c (t h)").bitcast(U32)
@@ -140,20 +144,19 @@ def tile_attend_gate_topk_kernel(tc, qT, k_words, k_scales, vT, vs, og, offs, ou
         v_ps_bf = v_ps[:].rearrange("s t c -> s (t c)").bitcast(BF16).rearrange("s (t e) -> s e t", t=PACK)
         v_codes = sb.tile([P, DV], U32, name="v_codes", align_bytes=64)
         v_sc = sb.tile([P, DV], U8, name="v_sc", align_bytes=64)
-        half = DV // 2
         for u in range(2):
-            cols = slice(u * half, (u + 1) * half)
+            cols = slice(u * HALF, (u + 1) * HALF)
             nc.scalar.copy(out=v_il[:, cols, :], in_=v_ps_bf[:, cols, :])
             nc.vector.quantize_mx(out=v_codes[:, cols].bitcast(FP8X4), scales=v_sc[:, cols],
                                   in_=v_il[:, cols, :].rearrange("s e t -> s (e t)"))
         gate = sb.tile([P, DV], F32, name="gate")
         nc.scalar.activation(out=gate[:], in_=th[:], func=ACT.Identity, bias=r_sum[:], scale=r_sum[:])
         for u, queue in enumerate((nc.sync, nc.scalar)):
-            cols = slice(u * half, (u + 1) * half)
-            y_ps = ps.tile([P, half], F32, name="y_ps%d" % u)
+            cols = slice(u * HALF, (u + 1) * HALF)
+            y_ps = ps.tile([P, HALF], F32, name="y_ps%d" % u)
             nc.tensor.matmul_mx(out=y_ps[:], lhsT=w_codes[:].bitcast(FP8X4), lhsT_scale=w_sc[:],
                                 rhs=v_codes[:, cols].bitcast(FP8X4), rhs_scale=v_sc[:, cols], start=True, stop=True)
-            res = sb.tile([P, half], F32, name="res%d" % u)
+            res = sb.tile([P, HALF], F32, name="res%d" % u)
             nc.vector.scalar_tensor_tensor(out=res[:], in0=y_ps[:], scalar=0.5, in1=gate[:, cols],
                                            op0=ALU.mult, op1=ALU.mult)
             queue.dma_start(out=out[0, :, cols], in_=res[:])

@@ -9,7 +9,6 @@ PACK = 4
 PASSES = D // (P * PACK)
 SCALE_ROWS = 4
 SECOND = 16
-V_CHUNK = 256
 HALF = DV // 2
 
 FLOPS = 2 * NQ * N * (D + DV)
@@ -31,91 +30,84 @@ def tile_attend_gate_topk_kernel(tc, qT, k_words, k_scales, vT, vs, og, offs, ou
     nc = tc.nc
     with ExitStack() as ctx:
         sb = ctx.enter_context(tc.tile_pool(name="sb", bufs=1))
+        reused = ctx.enter_context(tc.tile_pool(name="reused", bufs=1))
         ps = ctx.enter_context(tc.psum_pool(name="ps", bufs=1))
 
         offsets = sb.tile([P, N // 16], U16, name="offsets")
         vs_pool = sb.tile([P, T], F32, name="vs_pool")
         kw_pool = sb.tile([P, T], I32, name="kw_pool")
-        ks_pool = sb.tile([P, T], U8, name="ks_pool", tag="scales_then_words", align_bytes=64)
+        ks_pool = reused.tile([P, T], U8, name="ks_pool", offset=3584, align_bytes=64)
         ks_second = sb.tile([P, N], U8, name="ks_second", align_bytes=64)
         q_raw = [sb.tile([P, PACK, NQ], F32, name="q_raw%d" % o) for o in range(PASSES)]
-        v_raw = [sb.tile([P, 2, V_CHUNK], F32, name="v_raw%d" % i) for i in range(T // V_CHUNK)]
-        gate_in = sb.tile([P, DV], F32, name="gate_in")
+        v_raw0 = [sb.tile([P, T // 2], F32, name="v_raw0_%d" % i) for i in range(2)]
         ident = sb.tile([P, P], F32, name="ident")
 
-        nc.sync.dma_start(offsets[:], offs)
-        nc.sync.dma_start(out=vs_pool[P - 1:P, :], in_=vs[0:1, :])
-        nc.sync.dma_start(out=kw_pool[:], in_=k_words[0].rearrange("p t b -> p (t b)").bitcast(I32))
         ks_words = ks_pool[:].bitcast(I32)
         nc.vector.memset(ks_words, 0)
-        nc.vector.memset(vs_pool[0:P - 1, :], 0.0)
-        nc.vector.memset(ks_second[:].bitcast(I32), 0)
+        nc.sync.dma_start(offsets[:], offs)
+        kw_rows = k_words[0].rearrange("p t b -> p (t b)").bitcast(I32)
         ks_rows = k_scales.bitcast(I32).rearrange("o (quad r) w -> r quad o w", r=SCALE_ROWS)
-        for r in range(SCALE_ROWS):
-            nc.sync.dma_start(out=ks_words[r:P:SECOND, :], in_=ks_rows[r])
+        for r, queue in enumerate((nc.sync, nc.scalar, nc.sync, nc.scalar)):
+            queue.dma_start(out=ks_words[r:P:SECOND, :], in_=ks_rows[r])
+        nc.sync.dma_start(out=kw_pool[:], in_=kw_rows)
         q_rows = qT[0].rearrange("(o p j) q -> o p j q", o=PASSES, j=PACK)
         for o in range(PASSES):
             nc.sync.dma_start(out=q_raw[o][:], in_=q_rows[o])
-        v_rows = vT.rearrange("(c h) t -> c h t", h=2)
-        for i in range(T // V_CHUNK):
-            nc.sync.dma_start(out=v_raw[i][:], in_=v_rows[:, :, i * V_CHUNK:(i + 1) * V_CHUNK])
-        nc.sync.dma_start(out=gate_in[:], in_=og[0])
+        nc.sync.dma_start(out=v_raw0[0][:], in_=vT[0:HALF, 0:T // 2])
+        nc.sync.dma_start(out=v_raw0[1][:], in_=vT[0:HALF, T // 2:T])
+        nc.sync.dma_start(out=vs_pool[P - 1:P, :], in_=vs[0:1, :])
+        nc.vector.memset(vs_pool[0:P - 1, :], 0.0)
+        nc.vector.memset(ks_second[:].bitcast(I32), 0)
         make_identity(nc, ident[:])
-
-        vs_g = sb.tile([P, N], F32, name="vs_g")
-        nc.vector.tensor_copy(out=vs_g[:], in_=vs_pool[:].indirect(offsets[:]))
-        vs_ps = ps.tile([P, PACK, P], F32, name="vs_ps")
-        for t in range(PACK):
-            nc.tensor.transpose(vs_ps[:, t, :], vs_g[:, t:N:PACK], ident[:])
 
         ks_g = sb.tile([P, N], U8, name="ks_g", align_bytes=64)
         nc.vector.tensor_copy(out=ks_g[:], in_=ks_pool[:].indirect(offsets[:]))
         nc.sync.dma_start(out=ks_second[:].bitcast(I32)[0:P - SECOND, :], in_=ks_g[:].bitcast(I32)[SECOND:P, :])
-        kw_g = sb.tile([P, N], U32, name="kw_g", tag="scales_then_words", align_bytes=64)
+        gate_in = reused.tile([P, DV], F32, name="gate_in", offset=4096, align_bytes=64)
+        v_raw1 = reused.tile([P, T], F32, name="v_raw1", offset=0, align_bytes=64)
+        nc.sync.dma_start(out=gate_in[:], in_=og[0])
+        nc.sync.dma_start(out=v_raw1[:], in_=vT[HALF:DV, :])
+        kw_g = sb.tile([P, N], U32, name="kw_g", align_bytes=64)
         nc.vector.tensor_copy(out=kw_g[:], in_=kw_pool[:].bitcast(U32).indirect(offsets[:]))
 
-        q_il = sb.tile([P, PASSES, NQ, PACK], BF16, name="q_il", align_bytes=64)
-        q_by_query = [q_raw[o][:].rearrange("p j q -> p q j") for o in range(PASSES)]
-        nc.scalar.activation(out=q_il[:, 0, :, :], in_=q_by_query[0], func=ACT.Copy)
-        q_codes = sb.tile([P, PASSES * NQ], U32, name="q_codes", align_bytes=64)
-        q_sc = sb.tile([P, PASSES * NQ], U8, name="q_sc", align_bytes=64)
+        q_il = [sb.tile([P, NQ, PACK], BF16, name="q_il%d" % o, align_bytes=64) for o in range(PASSES)]
+        q_codes = [sb.tile([P, NQ], U32, name="q_codes%d" % o, align_bytes=64) for o in range(PASSES)]
+        q_sc = [sb.tile([P, NQ], U8, name="q_sc%d" % o, align_bytes=64) for o in range(PASSES)]
         k_op = sb.tile([P, PASSES, N], U16, name="k_op", align_bytes=64)
         kw_halves = kw_g[:].bitcast(U16).rearrange("p (n o) -> p o n", o=PASSES)
-
-        def quantise_queries(o):
-            cols = slice(o * NQ, (o + 1) * NQ)
-            nc.vector.quantize_mx(out=q_codes[:, cols].bitcast(FP8X4), scales=q_sc[:, cols],
-                                  in_=q_il[:, o, :, :].rearrange("p q j -> p (q j)"))
-
-        quantise_queries(0)
-        nc.vector.tensor_copy(out=q_il[:, 1, :, :], in_=q_by_query[1])
-        for o in range(PASSES):
-            nc.vector.tensor_copy(out=k_op[:, o, :], in_=kw_halves[:, o, :])
-        quantise_queries(1)
-
-        scores = ps.tile([P, N], F32, name="scores")
+        scores = ps.tile([P, N], F32, name="scores", tag="scores_then_values")
         for o, plane in enumerate((ks_g, ks_second)):
-            cols = slice(o * NQ, (o + 1) * NQ)
-            nc.tensor.matmul_mx(out=scores[:], lhsT=q_codes[:, cols].bitcast(FP8X4), lhsT_scale=q_sc[:, cols],
+            nc.scalar.activation(out=q_il[o][:], in_=q_raw[o][:].rearrange("p j q -> p q j"), func=ACT.Copy)
+            nc.vector.tensor_copy(out=k_op[:, o, :], in_=kw_halves[:, o, :])
+            nc.vector.quantize_mx(out=q_codes[o][:].bitcast(FP8X4), scales=q_sc[o][:],
+                                  in_=q_il[o][:].rearrange("p q j -> p (q j)"))
+            nc.tensor.matmul_mx(out=scores[:], lhsT=q_codes[o][:].bitcast(FP8X4), lhsT_scale=q_sc[o][:],
                                 rhs=k_op[:, o, :].bitcast(FP4X4), rhs_scale=plane[:],
                                 start=(o == 0), stop=(o == PASSES - 1))
 
+        vs_g = sb.tile([P, N], F32, name="vs_g")
+        nc.vector.tensor_copy(out=vs_g[:], in_=vs_pool[:].indirect(offsets[:]))
         vs_col = sb.tile([P, PACK], F32, name="vs_col")
-        nc.scalar.activation(out=vs_col[:], in_=vs_ps[:, :, P - 1], func=ACT.Copy)
+        nc.sync.dma_start(out=vs_col[:], in_=vs_g[P - 1:P, :])
 
-        v_pool = sb.tile([P, T, 2], BF16, name="v_pool", tag="v_chain", align_bytes=64)
-        for i in range(T // V_CHUNK):
-            nc.scalar.activation(out=v_pool[:, i * V_CHUNK:(i + 1) * V_CHUNK, :], in_=v_raw[i][:].rearrange("c h t -> c t h"), func=ACT.Copy)
+        v_bf0 = sb.tile([P, T], BF16, name="v_bf0", align_bytes=64)
+        for i in range(2):
+            nc.scalar.activation(out=v_bf0[:, i * T // 2:(i + 1) * T // 2], in_=v_raw0[i][:], func=ACT.Copy)
+        v_g = [sb.tile([P, N], BF16, name="v_g%d" % u, align_bytes=64) for u in range(2)]
+        nc.scalar.activation(out=v_g[0][:], in_=v_bf0[:].indirect(offsets[:]), func=ACT.Copy)
+        v_codes = sb.tile([P, DV], U32, name="v_codes", align_bytes=64)
 
-        v_g = sb.tile([P, PACK, P], U32, name="v_g", align_bytes=64)
-        v_window = v_pool[:].rearrange("c t h -> c (t h)").bitcast(U32)
-        nc.vector.tensor_copy(out=v_g[:].rearrange("c t s -> c s t"), in_=v_window.indirect(offsets[:]))
-        v_ps = ps.tile([P, PACK, P], F32, name="v_ps")
-        for t in range(PACK):
-            nc.tensor.transpose(v_ps[:, t, :], v_g[:, t, :].bitcast(F32), ident[:])
+        def turn_values(u, bank):
+            words = v_g[u][:].bitcast(F32)
+            for j in range(2):
+                nc.tensor.transpose(bank[:, j, :], words[:, j:N // 2:2], ident[:])
 
-        neg_m = sb.tile([P, 1], F32, name="neg_m", tag="v_chain", align_bytes=64)
+        v_ps0 = ps.tile([P, 2, P], F32, name="v_ps0")
+        turn_values(0, v_ps0)
+
+        neg_m = sb.tile([P, 1], F32, name="neg_m", tag="maximum_then_values", align_bytes=64)
         nc.vector.tensor_reduce(out=neg_m[:], in_=scores[:], axis=AXIS.X, op=ALU.max, negate=True)
+        nc.vector.tensor_copy(out=v_g[1][:], in_=v_raw1[:].indirect(offsets[:]))
         p_sb = sb.tile([P, PACK, P], F32, name="p_sb")
         l_half = [sb.tile([P, 1], F32, name="l_half%d" % u) for u in range(2)]
         s_by_t = scores[:].rearrange("q (s t) -> q t s", t=PACK)
@@ -125,32 +117,43 @@ def tile_attend_gate_topk_kernel(tc, qT, k_words, k_scales, vT, vs, og, offs, ou
                                  bias=neg_m[:], scale=1.0, accum_out=l_half[u][:])
             for t in (2 * u, 2 * u + 1):
                 nc.tensor.transpose(p_ps[:, t, :], p_sb[:, t, :], ident[:])
+        v_ps1 = ps.tile([P, 2, P], F32, name="v_ps1", tag="scores_then_values")
+        turn_values(1, v_ps1)
+
+        w_il = reused.tile([P, NQ, PACK], BF16, name="w_il", offset=0, align_bytes=64)
+        v_il = sb.tile([P, 2, HALF, 2], F32, name="v_il", tag="maximum_then_values", align_bytes=64)
+        v_sc = reused.tile([P, DV], U8, name="v_sc", offset=1088, align_bytes=64)
+
+        def quantise_values(u, bank):
+            cols = slice(u * HALF, (u + 1) * HALF)
+            nc.scalar.copy(out=v_il[:, u, :, :], in_=bank[:].rearrange("s j c -> s c j"))
+            nc.vector.quantize_mx(out=v_codes[:, cols].bitcast(FP8X4), scales=v_sc[:, cols],
+                                  in_=v_il[:, u, :, :].rearrange("s c j -> s (c j)").bitcast(BF16))
 
         l_sum = sb.tile([P, 1], F32, name="l_sum")
-        nc.vector.tensor_tensor(out=l_sum[:], in0=l_half[0][:], in1=l_half[1][:], op=ALU.add)
-        w_il = sb.tile([P, NQ, PACK], BF16, name="w_il", align_bytes=64)
-        nc.vector.tensor_tensor(out=w_il[:], in0=p_ps[:].rearrange("s t q -> s q t"),
-                                in1=vs_col[:].unsqueeze(1).to_broadcast([P, NQ, PACK]), op=ALU.mult)
-        r_sum = sb.tile([P, 1], F32, name="r_sum")
+        nc.scalar.activation(out=l_sum[:], in_=l_half[0][:], func=ACT.Identity, bias=l_half[1][:], scale=1.0)
+        r_sum = reused.tile([P, 1], F32, name="r_sum", offset=1024, align_bytes=64)
         nc.vector.reciprocal(out=r_sum[:], in_=l_sum[:])
-        w_codes = sb.tile([P, NQ], U32, name="w_codes", align_bytes=64)
-        w_sc = sb.tile([P, NQ], U8, name="w_sc", align_bytes=64)
-        nc.vector.quantize_mx(out=w_codes[:].bitcast(FP8X4), scales=w_sc[:],
-                              in_=w_il[:].rearrange("s q t -> s (q t)"))
 
+        quantise_values(0, v_ps0)
         th = sb.tile([P, DV], F32, name="th")
         nc.scalar.activation(out=th[:], in_=gate_in[:], func=ACT.Tanh, scale=0.5)
-        v_il = sb.tile([P, DV, PACK], BF16, name="v_il", tag="v_chain", align_bytes=64)
-        v_ps_bf = v_ps[:].rearrange("s t c -> s (t c)").bitcast(BF16).rearrange("s (t e) -> s e t", t=PACK)
-        v_codes = sb.tile([P, DV], U32, name="v_codes", align_bytes=64)
-        v_sc = sb.tile([P, DV], U8, name="v_sc", align_bytes=64)
-        for u in range(2):
-            cols = slice(u * HALF, (u + 1) * HALF)
-            nc.scalar.copy(out=v_il[:, cols, :], in_=v_ps_bf[:, cols, :])
-            nc.vector.quantize_mx(out=v_codes[:, cols].bitcast(FP8X4), scales=v_sc[:, cols],
-                                  in_=v_il[:, cols, :].rearrange("s e t -> s (e t)"))
         gate = sb.tile([P, DV], F32, name="gate")
         nc.scalar.activation(out=gate[:], in_=th[:], func=ACT.Identity, bias=r_sum[:], scale=r_sum[:])
+        w_codes = sb.tile([P, NQ], U32, name="w_codes", align_bytes=64)
+        w_sc = sb.tile([P, NQ], U8, name="w_sc", align_bytes=64)
+        query_halves = (slice(0, NQ // 2), slice(NQ // 2, NQ))
+        for rows in query_halves:
+            nc.vector.tensor_tensor(out=w_il[:, rows, :], in0=p_ps[:, :, rows].rearrange("s t q -> s q t"),
+                                    in1=vs_col[:].unsqueeze(1).to_broadcast([P, NQ // 2, PACK]), op=ALU.mult)
+
+        def quantise_weights(rows, codes):
+            nc.vector.quantize_mx(out=codes.bitcast(FP8X4), scales=w_sc[:, rows],
+                                  in_=w_il[:, rows, :].rearrange("s q t -> s (q t)"))
+
+        quantise_weights(query_halves[0], w_codes[:, query_halves[0]])
+        quantise_values(1, v_ps1)
+        quantise_weights(query_halves[1], w_codes[:, query_halves[1]])
         for u, queue in enumerate((nc.sync, nc.scalar)):
             cols = slice(u * HALF, (u + 1) * HALF)
             y_ps = ps.tile([P, HALF], F32, name="y_ps%d" % u)

@@ -37,7 +37,7 @@ def tile_attend_gate_topk_kernel(tc, qT, k_words, k_scales, vT, vs, og, offs, ou
         vs_pool = sb.tile([P, T], F32, name="vs_pool")
         kw_pool = sb.tile([P, T], I32, name="kw_pool")
         ks_pool = reused.tile([P, T], U8, name="ks_pool", offset=3584, align_bytes=64)
-        ks_second = sb.tile([P, N], U8, name="ks_second", align_bytes=64)
+        ks_second = sb.tile([P, N], U8, name="ks_second", tag="plane_then_identity", align_bytes=64)
         q_raw = [sb.tile([P, PACK, NQ], F32, name="q_raw%d" % o) for o in range(PASSES)]
         v_raw0 = [sb.tile([P, T // 2], F32, name="v_raw0_%d" % i) for i in range(2)]
         ident = sb.tile([P, P], F32, name="ident")
@@ -62,23 +62,28 @@ def tile_attend_gate_topk_kernel(tc, qT, k_words, k_scales, vT, vs, og, offs, ou
 
         ks_g = sb.tile([P, N], U8, name="ks_g", align_bytes=64)
         nc.vector.tensor_copy(out=ks_g[:], in_=ks_pool[:].indirect(offsets[:]))
-        nc.sync.dma_start(out=ks_second[:].bitcast(I32)[0:P - SECOND, :], in_=ks_g[:].bitcast(I32)[SECOND:P, :])
+        for lo, count in ((0, 64), (64, 32), (96, 16)):
+            nc.sync.dma_start(out=ks_second[:].bitcast(I32)[lo:lo + count, :],
+                              in_=ks_g[:].bitcast(I32)[lo + SECOND:lo + SECOND + count, :])
         gate_in = reused.tile([P, DV], F32, name="gate_in", offset=4096, align_bytes=64)
-        v_raw1 = reused.tile([P, T], F32, name="v_raw1", offset=0, align_bytes=64)
         nc.sync.dma_start(out=gate_in[:], in_=og[0])
+        v_raw1 = reused.tile([P, T], F32, name="v_raw1", offset=0, align_bytes=64)
         nc.sync.dma_start(out=v_raw1[:], in_=vT[HALF:DV, :])
-        kw_g = sb.tile([P, N], U32, name="kw_g", align_bytes=64)
-        nc.vector.tensor_copy(out=kw_g[:], in_=kw_pool[:].bitcast(U32).indirect(offsets[:]))
+        kw_g = [sb.tile([P, N // 2], U32, name="kw_g%d" % h, align_bytes=64) for h in range(2)]
+        for h in range(2):
+            nc.vector.tensor_copy(out=kw_g[h][:],
+                                  in_=kw_pool[:].bitcast(U32).indirect(offsets[:, h * N // 32:(h + 1) * N // 32]))
 
         q_il = [sb.tile([P, NQ, PACK], BF16, name="q_il%d" % o, align_bytes=64) for o in range(PASSES)]
         q_codes = [sb.tile([P, NQ], U32, name="q_codes%d" % o, align_bytes=64) for o in range(PASSES)]
         q_sc = [sb.tile([P, NQ], U8, name="q_sc%d" % o, align_bytes=64) for o in range(PASSES)]
         k_op = sb.tile([P, PASSES, N], U16, name="k_op", align_bytes=64)
-        kw_halves = kw_g[:].bitcast(U16).rearrange("p (n o) -> p o n", o=PASSES)
+        for h in range(2):
+            nc.vector.tensor_copy(out=k_op[:, :, h * N // 2:(h + 1) * N // 2],
+                                  in_=kw_g[h][:].bitcast(U16).rearrange("p (n o) -> p o n", o=PASSES))
         scores = ps.tile([P, N], F32, name="scores", tag="scores_then_values")
         for o, plane in enumerate((ks_g, ks_second)):
             nc.scalar.activation(out=q_il[o][:], in_=q_raw[o][:].rearrange("p j q -> p q j"), func=ACT.Copy)
-            nc.vector.tensor_copy(out=k_op[:, o, :], in_=kw_halves[:, o, :])
             nc.vector.quantize_mx(out=q_codes[o][:].bitcast(FP8X4), scales=q_sc[o][:],
                                   in_=q_il[o][:].rearrange("p q j -> p (q j)"))
             nc.tensor.matmul_mx(out=scores[:], lhsT=q_codes[o][:].bitcast(FP8X4), lhsT_scale=q_sc[o][:],
@@ -97,10 +102,13 @@ def tile_attend_gate_topk_kernel(tc, qT, k_words, k_scales, vT, vs, og, offs, ou
         nc.scalar.activation(out=v_g[0][:], in_=v_bf0[:].indirect(offsets[:]), func=ACT.Copy)
         v_codes = sb.tile([P, DV], U32, name="v_codes", align_bytes=64)
 
+        ident_v = sb.tile([P, P], F32, name="ident_v", tag="plane_then_identity", align_bytes=64)
+        nc.scalar.copy(out=ident_v[:], in_=ident[:])
+
         def turn_values(u, bank):
             words = v_g[u][:].bitcast(F32)
             for j in range(2):
-                nc.tensor.transpose(bank[:, j, :], words[:, j:N // 2:2], ident[:])
+                nc.tensor.transpose(bank[:, j, :], words[:, j:N // 2:2], ident_v[:])
 
         v_ps0 = ps.tile([P, 2, P], F32, name="v_ps0")
         turn_values(0, v_ps0)

@@ -46,10 +46,11 @@ def tile_attend_gate_topk_kernel(tc, qT, k_words, k_scales, vT, vs, og, offs, ou
         nc.vector.memset(ks_words, 0)
         nc.sync.dma_start(offsets[:], offs)
         kw_rows = k_words[0].rearrange("p t b -> p (t b)").bitcast(I32)
+        nc.scalar.dma_start(out=kw_pool[:, 0:T // 4], in_=kw_rows[:, 0:T // 4])
         ks_rows = k_scales.bitcast(I32).rearrange("o (quad r) w -> r quad o w", r=SCALE_ROWS)
         for r, queue in enumerate((nc.sync, nc.scalar, nc.sync, nc.scalar)):
             queue.dma_start(out=ks_words[r:P:SECOND, :], in_=ks_rows[r])
-        nc.sync.dma_start(out=kw_pool[:], in_=kw_rows)
+        nc.sync.dma_start(out=kw_pool[:, T // 4:T], in_=kw_rows[:, T // 4:T])
         q_rows = qT[0].rearrange("(o p j) q -> o p j q", o=PASSES, j=PACK)
         for o in range(PASSES):
             nc.sync.dma_start(out=q_raw[o][:], in_=q_rows[o])
@@ -66,9 +67,9 @@ def tile_attend_gate_topk_kernel(tc, qT, k_words, k_scales, vT, vs, og, offs, ou
             nc.sync.dma_start(out=ks_second[:].bitcast(I32)[lo:lo + count, :],
                               in_=ks_g[:].bitcast(I32)[lo + SECOND:lo + SECOND + count, :])
         gate_in = reused.tile([P, DV], F32, name="gate_in", offset=4096, align_bytes=64)
-        nc.sync.dma_start(out=gate_in[:], in_=og[0])
         v_raw1 = reused.tile([P, T], F32, name="v_raw1", offset=0, align_bytes=64)
         nc.sync.dma_start(out=v_raw1[:], in_=vT[HALF:DV, :])
+        nc.sync.dma_start(out=gate_in[:], in_=og[0])
         kw_g = [sb.tile([P, N // 2], U32, name="kw_g%d" % h, align_bytes=64) for h in range(2)]
         for h in range(2):
             nc.vector.tensor_copy(out=kw_g[h][:],
@@ -83,7 +84,8 @@ def tile_attend_gate_topk_kernel(tc, qT, k_words, k_scales, vT, vs, og, offs, ou
                                   in_=kw_g[h][:].bitcast(U16).rearrange("p (n o) -> p o n", o=PASSES))
         scores = ps.tile([P, N], F32, name="scores", tag="scores_then_values")
         for o, plane in enumerate((ks_g, ks_second)):
-            nc.scalar.activation(out=q_il[o][:], in_=q_raw[o][:].rearrange("p j q -> p q j"), func=ACT.Copy)
+            nc.scalar.activation(out=q_il[o][:].rearrange("p (c i) j -> p c j i", i=PACK),
+                                 in_=q_raw[o][:].rearrange("p j (c i) -> p c j i", i=PACK), func=ACT.Copy)
             nc.vector.quantize_mx(out=q_codes[o][:].bitcast(FP8X4), scales=q_sc[o][:],
                                   in_=q_il[o][:].rearrange("p q j -> p (q j)"))
             nc.tensor.matmul_mx(out=scores[:], lhsT=q_codes[o][:].bitcast(FP8X4), lhsT_scale=q_sc[o][:],
@@ -162,7 +164,7 @@ def tile_attend_gate_topk_kernel(tc, qT, k_words, k_scales, vT, vs, og, offs, ou
         quantise_weights(query_halves[0], w_codes[:, query_halves[0]])
         quantise_values(1, v_ps1)
         quantise_weights(query_halves[1], w_codes[:, query_halves[1]])
-        for u, queue in enumerate((nc.sync, nc.scalar)):
+        for u, queue in enumerate((nc.scalar, nc.sync)):
             cols = slice(u * HALF, (u + 1) * HALF)
             y_ps = ps.tile([P, HALF], F32, name="y_ps%d" % u)
             nc.tensor.matmul_mx(out=y_ps[:], lhsT=w_codes[:].bitcast(FP8X4), lhsT_scale=w_sc[:],

@@ -8,7 +8,8 @@ P = 128
 PACK = 4
 PASSES = D // (P * PACK)
 SCALE_ROWS = 4
-SECOND = 16
+QUADS = 4
+STAGED = 96
 HALF = DV // 2
 
 FLOPS = 2 * NQ * N * (D + DV)
@@ -37,20 +38,16 @@ def tile_attend_gate_topk_kernel(tc, qT, k_words, k_scales, vT, vs, og, offs, ou
         vs_pool = sb.tile([P, T], F32, name="vs_pool")
         kw_pool = sb.tile([P, T], I32, name="kw_pool")
         ks_pool = reused.tile([P, T], U8, name="ks_pool", offset=3584, align_bytes=64)
-        ks_second = sb.tile([P, N], U8, name="ks_second", tag="plane_then_identity", align_bytes=64)
+        planes = sb.tile([P, PASSES, N], U8, name="planes", tag="plane_then_identity", align_bytes=64)
         q_raw = [sb.tile([P, PACK, NQ], F32, name="q_raw%d" % o) for o in range(PASSES)]
         v_raw0 = [sb.tile([P, T // 2], F32, name="v_raw0_%d" % i) for i in range(2)]
         ident = sb.tile([P, P], F32, name="ident")
 
         ks_words = ks_pool[:].bitcast(I32)
-        nc.vector.memset(ks_words, 0)
         nc.sync.dma_start(offsets[:], offs)
-        kw_rows = k_words[0].rearrange("p t b -> p (t b)").bitcast(I32)
-        nc.scalar.dma_start(out=kw_pool[:, 0:T // 4], in_=kw_rows[:, 0:T // 4])
-        ks_rows = k_scales.bitcast(I32).rearrange("o (quad r) w -> r quad o w", r=SCALE_ROWS)
-        for r, queue in enumerate((nc.sync, nc.scalar, nc.sync, nc.scalar)):
-            queue.dma_start(out=ks_words[r:P:SECOND, :], in_=ks_rows[r])
-        nc.sync.dma_start(out=kw_pool[:, T // 4:T], in_=kw_rows[:, T // 4:T])
+        nc.scalar.dma_start(out=ks_words[STAGED:P, :], in_=k_scales.bitcast(I32).rearrange("o f w -> f o w"))
+        nc.vector.memset(ks_words[0:STAGED, :], 0)
+        nc.sync.dma_start(out=kw_pool[:], in_=k_words[0].rearrange("p t b -> p (t b)").bitcast(I32))
         q_rows = qT[0].rearrange("(o p j) q -> o p j q", o=PASSES, j=PACK)
         for o in range(PASSES):
             nc.sync.dma_start(out=q_raw[o][:], in_=q_rows[o])
@@ -58,14 +55,17 @@ def tile_attend_gate_topk_kernel(tc, qT, k_words, k_scales, vT, vs, og, offs, ou
         nc.sync.dma_start(out=v_raw0[1][:], in_=vT[0:HALF, T // 2:T])
         nc.sync.dma_start(out=vs_pool[P - 1:P, :], in_=vs[0:1, :])
         nc.vector.memset(vs_pool[0:P - 1, :], 0.0)
-        nc.vector.memset(ks_second[:].bitcast(I32), 0)
+        plane_words = planes[:].rearrange("p o n -> p (o n)").bitcast(I32)
+        nc.vector.memset(plane_words, 0)
         make_identity(nc, ident[:])
 
         ks_g = sb.tile([P, N], U8, name="ks_g", align_bytes=64)
         nc.vector.tensor_copy(out=ks_g[:], in_=ks_pool[:].indirect(offsets[:]))
-        for lo, count in ((0, 64), (64, 32), (96, 16)):
-            nc.sync.dma_start(out=ks_second[:].bitcast(I32)[lo:lo + count, :],
-                              in_=ks_g[:].bitcast(I32)[lo + SECOND:lo + SECOND + count, :])
+        rows_a_quad = SCALE_ROWS * PASSES
+        for quad in range(QUADS):
+            lo = STAGED + quad * rows_a_quad
+            nc.sync.dma_start(out=plane_words[32 * quad:32 * quad + SCALE_ROWS, :],
+                              in_=ks_g[:].bitcast(I32)[lo:lo + rows_a_quad, :])
         gate_in = reused.tile([P, DV], F32, name="gate_in", offset=4096, align_bytes=64)
         v_raw1 = reused.tile([P, T], F32, name="v_raw1", offset=0, align_bytes=64)
         nc.sync.dma_start(out=v_raw1[:], in_=vT[HALF:DV, :])
@@ -83,13 +83,13 @@ def tile_attend_gate_topk_kernel(tc, qT, k_words, k_scales, vT, vs, og, offs, ou
             nc.vector.tensor_copy(out=k_op[:, :, h * N // 2:(h + 1) * N // 2],
                                   in_=kw_g[h][:].bitcast(U16).rearrange("p (n o) -> p o n", o=PASSES))
         scores = ps.tile([P, N], F32, name="scores", tag="scores_then_values")
-        for o, plane in enumerate((ks_g, ks_second)):
+        for o in range(PASSES):
             nc.scalar.activation(out=q_il[o][:].rearrange("p (c i) j -> p c j i", i=PACK),
                                  in_=q_raw[o][:].rearrange("p j (c i) -> p c j i", i=PACK), func=ACT.Copy)
             nc.vector.quantize_mx(out=q_codes[o][:].bitcast(FP8X4), scales=q_sc[o][:],
                                   in_=q_il[o][:].rearrange("p q j -> p (q j)"))
             nc.tensor.matmul_mx(out=scores[:], lhsT=q_codes[o][:].bitcast(FP8X4), lhsT_scale=q_sc[o][:],
-                                rhs=k_op[:, o, :].bitcast(FP4X4), rhs_scale=plane[:],
+                                rhs=k_op[:, o, :].bitcast(FP4X4), rhs_scale=planes[:, o, :],
                                 start=(o == 0), stop=(o == PASSES - 1))
 
         vs_g = sb.tile([P, N], F32, name="vs_g")

@@ -12,6 +12,9 @@ QUADS = 4
 STAGED = 96
 HALF = DV // 2
 
+
+SPLIT = 384
+
 FLOPS = 2 * NQ * N * (D + DV)
 
 F32 = mybir.dt.float32
@@ -31,30 +34,33 @@ def tile_attend_gate_topk_kernel(tc, qT, k_words, k_scales, vT, vs, og, offs, ou
     nc = tc.nc
     with ExitStack() as ctx:
         sb = ctx.enter_context(tc.tile_pool(name="sb", bufs=1))
-        reused = ctx.enter_context(tc.tile_pool(name="reused", bufs=1))
         ps = ctx.enter_context(tc.psum_pool(name="ps", bufs=1))
 
         offsets = sb.tile([P, N // 16], U16, name="offsets")
-        vs_pool = sb.tile([P, T], F32, name="vs_pool")
+        ks_pool = sb.tile([P, T], U8, name="ks_pool", tag="scale_rows_then_values", align_bytes=64)
+        vs_pool = sb.tile([P, T], F32, name="vs_pool", tag="token_scales_then_gate", align_bytes=64)
         kw_pool = sb.tile([P, T], I32, name="kw_pool")
-        ks_pool = reused.tile([P, T], U8, name="ks_pool", offset=3584, align_bytes=64)
-        planes = sb.tile([P, PASSES, N], U8, name="planes", tag="plane_then_identity", align_bytes=64)
-        q_raw = [sb.tile([P, PACK, NQ], F32, name="q_raw%d" % o) for o in range(PASSES)]
-        v_raw0 = [sb.tile([P, T // 2], F32, name="v_raw0_%d" % i) for i in range(2)]
+        planes = sb.tile([P, PASSES, N], U8, name="planes", align_bytes=64)
+        q_raw = [sb.tile([P, PACK, NQ], F32, name="q_raw%d" % o, tag="queries%d" % o, align_bytes=64)
+                 for o in range(PASSES)]
+        v_raw0 = sb.tile([P, T], F32, name="v_raw0", align_bytes=64)
         ident = sb.tile([P, P], F32, name="ident")
 
         ks_words = ks_pool[:].bitcast(I32)
         nc.sync.dma_start(offsets[:], offs)
         nc.scalar.dma_start(out=ks_words[STAGED:P, :], in_=k_scales.bitcast(I32).rearrange("o f w -> f o w"))
+        nc.scalar.dma_start(out=vs_pool[P - 1:P, :], in_=vs[0:1, :])
+        one = sb.tile([P, 1], F32, name="one")
+        nc.vector.memset(one[:], 1.0)
+        minus_one = sb.tile([P, 1], F32, name="minus_one", tag="sign_then_values", align_bytes=64)
+        nc.scalar.activation(out=minus_one[:], in_=one[:], func=ACT.Copy, scale=-1.0)
         nc.vector.memset(ks_words[0:STAGED, :], 0)
+        nc.vector.memset(vs_pool[0:P - 1, :], 0.0)
         nc.sync.dma_start(out=kw_pool[:], in_=k_words[0].rearrange("p t b -> p (t b)").bitcast(I32))
         q_rows = qT[0].rearrange("(o p j) q -> o p j q", o=PASSES, j=PACK)
         for o in range(PASSES):
             nc.sync.dma_start(out=q_raw[o][:], in_=q_rows[o])
-        nc.sync.dma_start(out=v_raw0[0][:], in_=vT[0:HALF, 0:T // 2])
-        nc.sync.dma_start(out=v_raw0[1][:], in_=vT[0:HALF, T // 2:T])
-        nc.sync.dma_start(out=vs_pool[P - 1:P, :], in_=vs[0:1, :])
-        nc.vector.memset(vs_pool[0:P - 1, :], 0.0)
+        nc.sync.dma_start(out=v_raw0[:], in_=vT[0:HALF, :])
         plane_words = planes[:].rearrange("p o n -> p (o n)").bitcast(I32)
         nc.vector.memset(plane_words, 0)
         make_identity(nc, ident[:])
@@ -66,90 +72,94 @@ def tile_attend_gate_topk_kernel(tc, qT, k_words, k_scales, vT, vs, og, offs, ou
             lo = STAGED + quad * rows_a_quad
             nc.sync.dma_start(out=plane_words[32 * quad:32 * quad + SCALE_ROWS, :],
                               in_=ks_g[:].bitcast(I32)[lo:lo + rows_a_quad, :])
-        gate_in = reused.tile([P, DV], F32, name="gate_in", offset=4096, align_bytes=64)
-        v_raw1 = reused.tile([P, T], F32, name="v_raw1", offset=0, align_bytes=64)
+        v_raw1 = sb.tile([P, T], F32, name="v_raw1", tag="scale_rows_then_values", align_bytes=64)
         nc.sync.dma_start(out=v_raw1[:], in_=vT[HALF:DV, :])
-        nc.sync.dma_start(out=gate_in[:], in_=og[0])
+
         kw_g = [sb.tile([P, N // 2], U32, name="kw_g%d" % h, align_bytes=64) for h in range(2)]
         for h in range(2):
             nc.vector.tensor_copy(out=kw_g[h][:],
                                   in_=kw_pool[:].bitcast(U32).indirect(offsets[:, h * N // 32:(h + 1) * N // 32]))
 
+        def part_words(h, tag):
+            parted = sb.tile([P, PASSES, N // 2], U16, name="k_op%d" % h, tag=tag, align_bytes=64)
+            nc.vector.tensor_copy(out=parted[:], in_=kw_g[h][:].bitcast(U16).rearrange("p (n o) -> p o n", o=PASSES))
+            return parted
+
+        k_op = [part_words(0, "keys0")]
+
         q_il = [sb.tile([P, NQ, PACK], BF16, name="q_il%d" % o, align_bytes=64) for o in range(PASSES)]
         q_codes = [sb.tile([P, NQ], U32, name="q_codes%d" % o, align_bytes=64) for o in range(PASSES)]
         q_sc = [sb.tile([P, NQ], U8, name="q_sc%d" % o, align_bytes=64) for o in range(PASSES)]
-        k_op = sb.tile([P, PASSES, N], U16, name="k_op", align_bytes=64)
-        for h in range(2):
-            nc.vector.tensor_copy(out=k_op[:, :, h * N // 2:(h + 1) * N // 2],
-                                  in_=kw_g[h][:].bitcast(U16).rearrange("p (n o) -> p o n", o=PASSES))
-        scores = ps.tile([P, N], F32, name="scores", tag="scores_then_values")
         for o in range(PASSES):
             nc.scalar.activation(out=q_il[o][:].rearrange("p (c i) j -> p c j i", i=PACK),
                                  in_=q_raw[o][:].rearrange("p j (c i) -> p c j i", i=PACK), func=ACT.Copy)
             nc.vector.quantize_mx(out=q_codes[o][:].bitcast(FP8X4), scales=q_sc[o][:],
                                   in_=q_il[o][:].rearrange("p q j -> p (q j)"))
-            nc.tensor.matmul_mx(out=scores[:], lhsT=q_codes[o][:].bitcast(FP8X4), lhsT_scale=q_sc[o][:],
-                                rhs=k_op[:, o, :].bitcast(FP4X4), rhs_scale=planes[:, o, :],
-                                start=(o == 0), stop=(o == PASSES - 1))
+
+        k_op.append(part_words(1, "queries1"))
 
         vs_g = sb.tile([P, N], F32, name="vs_g")
-        nc.vector.tensor_copy(out=vs_g[:], in_=vs_pool[:].indirect(offsets[:]))
-        vs_col = sb.tile([P, PACK], F32, name="vs_col")
+        nc.scalar.activation(out=vs_g[:], in_=vs_pool[:].indirect(offsets[:]), func=ACT.Copy)
+        vs_col = sb.tile([P, PACK], F32, name="vs_col", tag="scales_then_codes", align_bytes=64)
         nc.sync.dma_start(out=vs_col[:], in_=vs_g[P - 1:P, :])
+        gate_in = sb.tile([P, DV], F32, name="gate_in", tag="token_scales_then_gate", align_bytes=64)
+        nc.sync.dma_start(out=gate_in[:], in_=og[0])
 
-        v_bf0 = sb.tile([P, T], BF16, name="v_bf0", align_bytes=64)
-        for i in range(2):
-            nc.scalar.activation(out=v_bf0[:, i * T // 2:(i + 1) * T // 2], in_=v_raw0[i][:], func=ACT.Copy)
-        v_g = [sb.tile([P, N], BF16, name="v_g%d" % u, align_bytes=64) for u in range(2)]
-        nc.scalar.activation(out=v_g[0][:], in_=v_bf0[:].indirect(offsets[:]), func=ACT.Copy)
-        v_codes = sb.tile([P, DV], U32, name="v_codes", align_bytes=64)
+        neg_s = sb.tile([P, PACK, P], F32, name="neg_s")
+        neg_m = [sb.tile([P, 1], F32, name="neg_m%d" % h) for h in range(2)]
+        for h in range(2):
+            scores = ps.tile([P, N // 2], F32, name="scores%d" % h, tag="bank%d" % h)
+            for o in range(PASSES):
+                nc.tensor.matmul_mx(out=scores[:], lhsT=q_codes[o][:].bitcast(FP8X4), lhsT_scale=q_sc[o][:],
+                                    rhs=k_op[h][:, o, :].bitcast(FP4X4),
+                                    rhs_scale=planes[:, o, h * N // 2:(h + 1) * N // 2],
+                                    start=(o == 0), stop=(o == PASSES - 1))
+            nc.vector.tensor_scalar(out=neg_s[:, :, h * P // 2:(h + 1) * P // 2],
+                                    in0=scores[:].rearrange("q (s t) -> q t s", t=PACK),
+                                    scalar1=-1.0, scalar2=neg_m[0][:] if h else None, op0=ALU.mult, op1=ALU.min,
+                                    accum_out=neg_m[h][:])
 
-        ident_v = sb.tile([P, P], F32, name="ident_v", tag="plane_then_identity", align_bytes=64)
-        nc.scalar.copy(out=ident_v[:], in_=ident[:])
+        v_g0 = sb.tile([P, N], BF16, name="v_g0", align_bytes=64)
+        nc.vector.tensor_copy(out=v_g0[:, 0:N // 2], in_=v_raw0[:].indirect(offsets[:, 0:N // 32]))
+        nc.scalar.activation(out=v_g0[:, N // 2:N], in_=v_raw0[:].indirect(offsets[:, N // 32:N // 16]), func=ACT.Copy)
+        v_g1 = sb.tile([P, N], BF16, name="v_g1", tag="queries1", align_bytes=64)
+        nc.vector.tensor_copy(out=v_g1[:, 0:SPLIT], in_=v_raw1[:].indirect(offsets[:, 0:SPLIT // 16]))
+        nc.scalar.activation(out=v_g1[:, SPLIT:N], in_=v_raw1[:].indirect(offsets[:, SPLIT // 16:N // 16]),
+                             func=ACT.Copy)
+        v_sc = sb.tile([P, DV], U8, name="v_sc", align_bytes=64)
 
-        def turn_values(u, bank):
-            words = v_g[u][:].bitcast(F32)
+        def turn_values(u, gathered):
+            bank = ps.tile([P, 2, P], F32, name="v_ps%d" % u, tag="bank0")
+            words = gathered[:].bitcast(F32)
             for j in range(2):
-                nc.tensor.transpose(bank[:, j, :], words[:, j:N // 2:2], ident_v[:])
+                nc.tensor.transpose(bank[:, j, :], words[:, j:N // 2:2], ident[:])
+            return bank[:].rearrange("s j c -> s c j")
 
-        v_ps0 = ps.tile([P, 2, P], F32, name="v_ps0")
-        turn_values(0, v_ps0)
+        def quantise_values(u, v_il, codes):
+            nc.vector.quantize_mx(out=codes[:].bitcast(FP8X4), scales=v_sc[:, u * HALF:(u + 1) * HALF],
+                                  in_=v_il[:].rearrange("s c j -> s (c j)").bitcast(BF16))
 
-        neg_m = sb.tile([P, 1], F32, name="neg_m", tag="maximum_then_values", align_bytes=64)
-        nc.vector.tensor_reduce(out=neg_m[:], in_=scores[:], axis=AXIS.X, op=ALU.max, negate=True)
-        nc.vector.tensor_copy(out=v_g[1][:], in_=v_raw1[:].indirect(offsets[:]))
-        p_sb = sb.tile([P, PACK, P], F32, name="p_sb")
+        turned0 = turn_values(0, v_g0)
+
+        p_sb = [sb.tile([P, 2, P], F32, name="p_sb%d" % u) for u in range(2)]
         l_half = [sb.tile([P, 1], F32, name="l_half%d" % u) for u in range(2)]
-        s_by_t = scores[:].rearrange("q (s t) -> q t s", t=PACK)
         p_ps = ps.tile([P, PACK, NQ], F32, name="p_ps")
         for u in range(2):
-            nc.scalar.activation(out=p_sb[:, 2 * u:2 * u + 2, :], in_=s_by_t[:, 2 * u:2 * u + 2, :], func=ACT.Exp,
-                                 bias=neg_m[:], scale=1.0, accum_out=l_half[u][:])
-            for t in (2 * u, 2 * u + 1):
-                nc.tensor.transpose(p_ps[:, t, :], p_sb[:, t, :], ident[:])
-        v_ps1 = ps.tile([P, 2, P], F32, name="v_ps1", tag="scores_then_values")
-        turn_values(1, v_ps1)
+            nc.scalar.activation(out=p_sb[u][:], in_=neg_s[:, 2 * u:2 * u + 2, :], func=ACT.Exp,
+                                 bias=neg_m[1][:], scale=-1.0 if u else minus_one[:], accum_out=l_half[u][:])
+            for j in range(2):
+                nc.tensor.transpose(p_ps[:, 2 * u + j, :], p_sb[u][:, j, :], ident[:])
 
-        w_il = reused.tile([P, NQ, PACK], BF16, name="w_il", offset=0, align_bytes=64)
-        v_il = sb.tile([P, 2, HALF, 2], F32, name="v_il", tag="maximum_then_values", align_bytes=64)
-        v_sc = reused.tile([P, DV], U8, name="v_sc", offset=1088, align_bytes=64)
-
-        def quantise_values(u, bank):
-            cols = slice(u * HALF, (u + 1) * HALF)
-            nc.scalar.copy(out=v_il[:, u, :, :], in_=bank[:].rearrange("s j c -> s c j"))
-            nc.vector.quantize_mx(out=v_codes[:, cols].bitcast(FP8X4), scales=v_sc[:, cols],
-                                  in_=v_il[:, u, :, :].rearrange("s c j -> s (c j)").bitcast(BF16))
-
+        v_il0 = sb.tile([P, HALF, 2], F32, name="v_il0", tag="sign_then_values", align_bytes=64)
+        nc.scalar.copy(out=v_il0[:], in_=turned0)
+        v_codes0 = sb.tile([P, HALF], U32, name="v_codes0", align_bytes=64)
+        quantise_values(0, v_il0, v_codes0)
+        v_il1 = sb.tile([P, HALF, 2], F32, name="v_il1", align_bytes=64)
+        nc.scalar.copy(out=v_il1[:], in_=turn_values(1, v_g1))
         l_sum = sb.tile([P, 1], F32, name="l_sum")
         nc.scalar.activation(out=l_sum[:], in_=l_half[0][:], func=ACT.Identity, bias=l_half[1][:], scale=1.0)
-        r_sum = reused.tile([P, 1], F32, name="r_sum", offset=1024, align_bytes=64)
-        nc.vector.reciprocal(out=r_sum[:], in_=l_sum[:])
 
-        quantise_values(0, v_ps0)
-        th = sb.tile([P, DV], F32, name="th")
-        nc.scalar.activation(out=th[:], in_=gate_in[:], func=ACT.Tanh, scale=0.5)
-        gate = sb.tile([P, DV], F32, name="gate")
-        nc.scalar.activation(out=gate[:], in_=th[:], func=ACT.Identity, bias=r_sum[:], scale=r_sum[:])
+        w_il = sb.tile([P, NQ, PACK], BF16, name="w_il", tag="weights_then_reciprocal", align_bytes=64)
         w_codes = sb.tile([P, NQ], U32, name="w_codes", align_bytes=64)
         w_sc = sb.tile([P, NQ], U8, name="w_sc", align_bytes=64)
         query_halves = (slice(0, NQ // 2), slice(NQ // 2, NQ))
@@ -157,19 +167,28 @@ def tile_attend_gate_topk_kernel(tc, qT, k_words, k_scales, vT, vs, og, offs, ou
             nc.vector.tensor_tensor(out=w_il[:, rows, :], in0=p_ps[:, :, rows].rearrange("s t q -> s q t"),
                                     in1=vs_col[:].unsqueeze(1).to_broadcast([P, NQ // 2, PACK]), op=ALU.mult)
 
-        def quantise_weights(rows, codes):
-            nc.vector.quantize_mx(out=codes.bitcast(FP8X4), scales=w_sc[:, rows],
+        def quantise_weights(rows):
+            nc.vector.quantize_mx(out=w_codes[:, rows].bitcast(FP8X4), scales=w_sc[:, rows],
                                   in_=w_il[:, rows, :].rearrange("s q t -> s (q t)"))
 
-        quantise_weights(query_halves[0], w_codes[:, query_halves[0]])
-        quantise_values(1, v_ps1)
-        quantise_weights(query_halves[1], w_codes[:, query_halves[1]])
+        quantise_weights(query_halves[0])
+        quantise_weights(query_halves[1])
+        v_codes1 = sb.tile([P, HALF], U32, name="v_codes1", tag="scales_then_codes", align_bytes=64)
+        quantise_values(1, v_il1, v_codes1)
+        v_codes = (v_codes0, v_codes1)
+
+        th = sb.tile([P, DV], F32, name="th")
+        nc.scalar.activation(out=th[:], in_=gate_in[:], func=ACT.Tanh, scale=0.5)
+        gate = sb.tile([P, DV], F32, name="gate")
+        nc.scalar.activation(out=gate[:], in_=th[:], func=ACT.Copy, bias=0.5, scale=0.5)
+        r_sum = sb.tile([P, 1], F32, name="r_sum", tag="weights_then_reciprocal", align_bytes=64)
+        nc.vector.reciprocal(out=r_sum[:], in_=l_sum[:])
         for u, queue in enumerate((nc.scalar, nc.sync)):
             cols = slice(u * HALF, (u + 1) * HALF)
             y_ps = ps.tile([P, HALF], F32, name="y_ps%d" % u)
             nc.tensor.matmul_mx(out=y_ps[:], lhsT=w_codes[:].bitcast(FP8X4), lhsT_scale=w_sc[:],
-                                rhs=v_codes[:, cols].bitcast(FP8X4), rhs_scale=v_sc[:, cols], start=True, stop=True)
+                                rhs=v_codes[u][:].bitcast(FP8X4), rhs_scale=v_sc[:, cols], start=True, stop=True)
             res = sb.tile([P, HALF], F32, name="res%d" % u)
-            nc.vector.scalar_tensor_tensor(out=res[:], in0=y_ps[:], scalar=0.5, in1=gate[:, cols],
+            nc.vector.scalar_tensor_tensor(out=res[:], in0=y_ps[:], scalar=r_sum[:], in1=gate[:, cols],
                                            op0=ALU.mult, op1=ALU.mult)
             queue.dma_start(out=out[0, :, cols], in_=res[:])

@@ -12,9 +12,6 @@ QUADS = 4
 STAGED = 96
 HALF = DV // 2
 
-
-SPLIT = 384
-
 FLOPS = 2 * NQ * N * (D + DV)
 
 F32 = mybir.dt.float32
@@ -27,7 +24,6 @@ FP8X4 = mybir.dt.float8_e4m3fn_x4
 FP4X4 = mybir.dt.float4_e2m1fn_x4
 ACT = mybir.ActivationFunctionType
 ALU = mybir.AluOpType
-AXIS = mybir.AxisListType
 
 
 def tile_attend_gate_topk_kernel(tc, qT, k_words, k_scales, vT, vs, og, offs, out):
@@ -122,26 +118,25 @@ def tile_attend_gate_topk_kernel(tc, qT, k_words, k_scales, vT, vs, og, offs, ou
         v_g0 = sb.tile([P, N], BF16, name="v_g0", align_bytes=64)
         nc.vector.tensor_copy(out=v_g0[:, 0:N // 2], in_=v_raw0[:].indirect(offsets[:, 0:N // 32]))
         nc.scalar.activation(out=v_g0[:, N // 2:N], in_=v_raw0[:].indirect(offsets[:, N // 32:N // 16]), func=ACT.Copy)
-        v_g1 = sb.tile([P, N], BF16, name="v_g1", tag="queries1", align_bytes=64)
-        nc.vector.tensor_copy(out=v_g1[:, 0:SPLIT], in_=v_raw1[:].indirect(offsets[:, 0:SPLIT // 16]))
-        nc.scalar.activation(out=v_g1[:, SPLIT:N], in_=v_raw1[:].indirect(offsets[:, SPLIT // 16:N // 16]),
-                             func=ACT.Copy)
+        v_g1 = sb.tile([P, 2, P, 2], BF16, name="v_g1", tag="queries1", align_bytes=64)
+        nc.vector.tensor_copy(out=v_g1[:].rearrange("c j s e -> c s j e"), in_=v_raw1[:].indirect(offsets[:]))
         v_sc = sb.tile([P, DV], U8, name="v_sc", align_bytes=64)
 
-        def turn_values(u, gathered):
+        def turn_values(u, word_pairs):
             bank = ps.tile([P, 2, P], F32, name="v_ps%d" % u, tag="bank0")
-            words = gathered[:].bitcast(F32)
             for j in range(2):
-                nc.tensor.transpose(bank[:, j, :], words[:, j:N // 2:2], ident[:])
+                nc.tensor.transpose(bank[:, j, :], word_pairs[j], ident[:])
             return bank[:].rearrange("s j c -> s c j")
 
         def quantise_values(u, v_il, codes):
             nc.vector.quantize_mx(out=codes[:].bitcast(FP8X4), scales=v_sc[:, u * HALF:(u + 1) * HALF],
                                   in_=v_il[:].rearrange("s c j -> s (c j)").bitcast(BF16))
 
-        turned0 = turn_values(0, v_g0)
+        words0 = v_g0[:].bitcast(F32)
+        words1 = v_g1[:].rearrange("c j s e -> c (j s e)").bitcast(F32)
+        turned0 = turn_values(0, [words0[:, j:N // 2:2] for j in range(2)])
 
-        p_sb = [sb.tile([P, 2, P], F32, name="p_sb%d" % u) for u in range(2)]
+        p_sb = [sb.tile([P, 2, P], F32, name="p_sb%d" % u, tag="exps%d" % u, align_bytes=64) for u in range(2)]
         l_half = [sb.tile([P, 1], F32, name="l_half%d" % u) for u in range(2)]
         p_ps = ps.tile([P, PACK, NQ], F32, name="p_ps")
         for u in range(2):
@@ -152,10 +147,8 @@ def tile_attend_gate_topk_kernel(tc, qT, k_words, k_scales, vT, vs, og, offs, ou
 
         v_il0 = sb.tile([P, HALF, 2], F32, name="v_il0", tag="sign_then_values", align_bytes=64)
         nc.scalar.copy(out=v_il0[:], in_=turned0)
-        v_codes0 = sb.tile([P, HALF], U32, name="v_codes0", align_bytes=64)
-        quantise_values(0, v_il0, v_codes0)
         v_il1 = sb.tile([P, HALF, 2], F32, name="v_il1", align_bytes=64)
-        nc.scalar.copy(out=v_il1[:], in_=turn_values(1, v_g1))
+        nc.scalar.copy(out=v_il1[:], in_=turn_values(1, [words1[:, j * P:(j + 1) * P] for j in range(2)]))
         l_sum = sb.tile([P, 1], F32, name="l_sum")
         nc.scalar.activation(out=l_sum[:], in_=l_half[0][:], func=ACT.Identity, bias=l_half[1][:], scale=1.0)
 
@@ -172,6 +165,8 @@ def tile_attend_gate_topk_kernel(tc, qT, k_words, k_scales, vT, vs, og, offs, ou
                                   in_=w_il[:, rows, :].rearrange("s q t -> s (q t)"))
 
         quantise_weights(query_halves[0])
+        v_codes0 = sb.tile([P, HALF], U32, name="v_codes0", tag="exps1", align_bytes=64)
+        quantise_values(0, v_il0, v_codes0)
         quantise_weights(query_halves[1])
         v_codes1 = sb.tile([P, HALF], U32, name="v_codes1", tag="scales_then_codes", align_bytes=64)
         quantise_values(1, v_il1, v_codes1)

@@ -11,6 +11,7 @@ SCALE_ROWS = 4
 QUADS = 4
 STAGED = 96
 HALF = DV // 2
+SPLIT = 384
 
 FLOPS = 2 * NQ * N * (D + DV)
 
@@ -119,7 +120,13 @@ def tile_attend_gate_topk_kernel(tc, qT, k_words, k_scales, vT, vs, og, offs, ou
         nc.vector.tensor_copy(out=v_g0[:, 0:N // 2], in_=v_raw0[:].indirect(offsets[:, 0:N // 32]))
         nc.scalar.activation(out=v_g0[:, N // 2:N], in_=v_raw0[:].indirect(offsets[:, N // 32:N // 16]), func=ACT.Copy)
         v_g1 = sb.tile([P, 2, P, 2], BF16, name="v_g1", tag="queries1", align_bytes=64)
-        nc.vector.tensor_copy(out=v_g1[:].rearrange("c j s e -> c s j e"), in_=v_raw1[:].indirect(offsets[:]))
+        nc.vector.tensor_copy(out=v_g1[:, :, 0:SPLIT // PACK, :].rearrange("c j s e -> c s j e"),
+                              in_=v_raw1[:].indirect(offsets[:, 0:SPLIT // 16]))
+        v_rest = sb.tile([P, N - SPLIT], BF16, name="v_rest", align_bytes=64)
+        nc.scalar.activation(out=v_rest[:], in_=v_raw1[:].indirect(offsets[:, SPLIT // 16:N // 16]), func=ACT.Copy)
+        nc.gpsimd.tensor_copy(
+            out=v_g1[:].rearrange("c j s e -> c (j s e)").bitcast(I32).rearrange("c (j s) -> c j s", j=2)[:, :, SPLIT // PACK:P],
+            in_=v_rest[:].bitcast(I32).rearrange("c (s j) -> c j s", j=2))
         v_sc = sb.tile([P, DV], U8, name="v_sc", align_bytes=64)
 
         def turn_values(u, word_pairs):

@@ -38,8 +38,9 @@ def tile_attend_gate_topk_kernel(tc, qT, k_words, k_scales, vT, vs, og, offs, ou
         vs_pool = sb.tile([P, T], F32, name="vs_pool", tag="token_scales_then_gate", align_bytes=64)
         kw_pool = sb.tile([P, T], I32, name="kw_pool")
         planes = sb.tile([P, PASSES, N], U8, name="planes", align_bytes=64)
-        q_raw = [sb.tile([P, PACK, NQ], F32, name="q_raw%d" % o, tag="queries%d" % o, align_bytes=64)
-                 for o in range(PASSES)]
+        scales_and_queries = sb.tile([P, N // 2 + PACK * NQ], F32, name="scales_and_queries", align_bytes=64)
+        q_raw1 = sb.tile([P, PACK, NQ], F32, name="q_raw1", tag="queries1", align_bytes=64)
+        q_raw = [scales_and_queries[:, N // 2:].rearrange("p (j q) -> p j q", j=PACK), q_raw1[:]]
         v_raw0 = sb.tile([P, T], F32, name="v_raw0", align_bytes=64)
         ident = sb.tile([P, P], F32, name="ident")
 
@@ -56,7 +57,7 @@ def tile_attend_gate_topk_kernel(tc, qT, k_words, k_scales, vT, vs, og, offs, ou
         nc.sync.dma_start(out=kw_pool[:], in_=k_words[0].rearrange("p t b -> p (t b)").bitcast(I32))
         q_rows = qT[0].rearrange("(o p j) q -> o p j q", o=PASSES, j=PACK)
         for o in range(PASSES):
-            nc.sync.dma_start(out=q_raw[o][:], in_=q_rows[o])
+            nc.sync.dma_start(out=q_raw[o], in_=q_rows[o])
         nc.sync.dma_start(out=v_raw0[:], in_=vT[0:HALF, :])
         plane_words = planes[:].rearrange("p o n -> p (o n)").bitcast(I32)
         nc.vector.memset(plane_words, 0)
@@ -89,14 +90,16 @@ def tile_attend_gate_topk_kernel(tc, qT, k_words, k_scales, vT, vs, og, offs, ou
         q_sc = [sb.tile([P, NQ], U8, name="q_sc%d" % o, align_bytes=64) for o in range(PASSES)]
         for o in range(PASSES):
             nc.scalar.activation(out=q_il[o][:].rearrange("p (c i) j -> p c j i", i=PACK),
-                                 in_=q_raw[o][:].rearrange("p j (c i) -> p c j i", i=PACK), func=ACT.Copy)
+                                 in_=q_raw[o].rearrange("p j (c i) -> p c j i", i=PACK), func=ACT.Copy)
             nc.vector.quantize_mx(out=q_codes[o][:].bitcast(FP8X4), scales=q_sc[o][:],
                                   in_=q_il[o][:].rearrange("p q j -> p (q j)"))
 
         k_op.append(part_words(1, "queries1"))
 
-        vs_g = sb.tile([P, N], F32, name="vs_g")
-        nc.scalar.activation(out=vs_g[:], in_=vs_pool[:].indirect(offsets[:]), func=ACT.Copy)
+        vs_g = scales_and_queries[:, 0:N]
+        for h in range(2):
+            nc.scalar.activation(out=vs_g[:, h * N // 2:(h + 1) * N // 2], func=ACT.Copy,
+                                 in_=vs_pool[:].indirect(offsets[:, h * N // 32:(h + 1) * N // 32]))
         vs_col = sb.tile([P, PACK], F32, name="vs_col", tag="scales_then_codes", align_bytes=64)
         nc.sync.dma_start(out=vs_col[:], in_=vs_g[P - 1:P, :])
         gate_in = sb.tile([P, DV], F32, name="gate_in", tag="token_scales_then_gate", align_bytes=64)

@@ -11,7 +11,8 @@ SCALE_ROWS = 4
 QUADS = 4
 STAGED = 96
 HALF = DV // 2
-SPLIT = 384
+SHARE = 288
+SPLIT = 448
 
 FLOPS = 2 * NQ * N * (D + DV)
 
@@ -120,8 +121,8 @@ def tile_attend_gate_topk_kernel(tc, qT, k_words, k_scales, vT, vs, og, offs, ou
                                     accum_out=neg_m[h][:])
 
         v_g0 = sb.tile([P, N], BF16, name="v_g0", align_bytes=64)
-        nc.vector.tensor_copy(out=v_g0[:, 0:N // 2], in_=v_raw0[:].indirect(offsets[:, 0:N // 32]))
-        nc.scalar.activation(out=v_g0[:, N // 2:N], in_=v_raw0[:].indirect(offsets[:, N // 32:N // 16]), func=ACT.Copy)
+        nc.vector.tensor_copy(out=v_g0[:, 0:SHARE], in_=v_raw0[:].indirect(offsets[:, 0:SHARE // 16]))
+        nc.scalar.activation(out=v_g0[:, SHARE:N], in_=v_raw0[:].indirect(offsets[:, SHARE // 16:N // 16]), func=ACT.Copy)
         v_g1 = sb.tile([P, 2, P, 2], BF16, name="v_g1", tag="queries1", align_bytes=64)
         nc.vector.tensor_copy(out=v_g1[:, :, 0:SPLIT // PACK, :].rearrange("c j s e -> c s j e"),
                               in_=v_raw1[:].indirect(offsets[:, 0:SPLIT // 16]))

@@ -79,23 +79,30 @@ def tile_attend_gate_topk_kernel(tc, qT, k_words, k_scales, vT, vs, og, offs, ou
             nc.vector.tensor_copy(out=kw_g[h][:],
                                   in_=kw_pool[:].bitcast(U32).indirect(offsets[:, h * N // 32:(h + 1) * N // 32]))
 
-        def part_words(h, tag):
-            parted = sb.tile([P, PASSES, N // 2], U16, name="k_op%d" % h, tag=tag, align_bytes=64)
-            nc.vector.tensor_copy(out=parted[:], in_=kw_g[h][:].bitcast(U16).rearrange("p (n o) -> p o n", o=PASSES))
-            return parted
+        def word_halves(h):
+            return kw_g[h][:].bitcast(U16).rearrange("p (n o) -> p o n", o=PASSES)
 
-        k_op = [part_words(0, "keys0")]
+        first_keys = sb.tile([P, PASSES, N // 2], U16, name="first_keys", align_bytes=64)
+        nc.vector.tensor_copy(out=first_keys[:], in_=word_halves(0))
 
         q_il = [sb.tile([P, NQ, PACK], BF16, name="q_il%d" % o, align_bytes=64) for o in range(PASSES)]
         q_codes = [sb.tile([P, NQ], U32, name="q_codes%d" % o, align_bytes=64) for o in range(PASSES)]
         q_sc = [sb.tile([P, NQ], U8, name="q_sc%d" % o, align_bytes=64) for o in range(PASSES)]
-        for o in range(PASSES):
-            nc.scalar.activation(out=q_il[o][:].rearrange("p (c i) j -> p c j i", i=PACK),
-                                 in_=q_raw[o].rearrange("p j (c i) -> p c j i", i=PACK), func=ACT.Copy)
-            nc.vector.quantize_mx(out=q_codes[o][:].bitcast(FP8X4), scales=q_sc[o][:],
-                                  in_=q_il[o][:].rearrange("p q j -> p (q j)"))
 
-        k_op.append(part_words(1, "queries1"))
+        def quantise_queries(o, rows):
+            nc.scalar.activation(out=q_il[o][:, rows, :].rearrange("p (c i) j -> p c j i", i=PACK),
+                                 in_=q_raw[o][:, :, rows].rearrange("p j (c i) -> p c j i", i=PACK), func=ACT.Copy)
+            nc.vector.quantize_mx(out=q_codes[o][:, rows].bitcast(FP8X4), scales=q_sc[o][:, rows],
+                                  in_=q_il[o][:, rows, :].rearrange("p q j -> p (q j)"))
+
+        query_halves = (slice(0, NQ // 2), slice(NQ // 2, NQ))
+        quantise_queries(0, slice(0, NQ))
+        quantise_queries(1, query_halves[0])
+        quantise_queries(1, query_halves[1])
+        second_keys = sb.tile([P, PASSES, N // 2], U16, name="second_keys", tag="queries1", align_bytes=64)
+        for o in range(PASSES):
+            nc.vector.tensor_copy(out=second_keys[:, o, :], in_=word_halves(1)[:, o, :])
+        k_op = (first_keys, second_keys)
 
         vs_g = scales_and_queries[:, 0:N]
         for h in range(2):
@@ -166,7 +173,6 @@ def tile_attend_gate_topk_kernel(tc, qT, k_words, k_scales, vT, vs, og, offs, ou
         w_il = sb.tile([P, NQ, PACK], BF16, name="w_il", tag="weights_then_reciprocal", align_bytes=64)
         w_codes = sb.tile([P, NQ], U32, name="w_codes", align_bytes=64)
         w_sc = sb.tile([P, NQ], U8, name="w_sc", align_bytes=64)
-        query_halves = (slice(0, NQ // 2), slice(NQ // 2, NQ))
         for rows in query_halves:
             nc.vector.tensor_tensor(out=w_il[:, rows, :], in0=p_ps[:, :, rows].rearrange("s t q -> s q t"),
                                     in1=vs_col[:].unsqueeze(1).to_broadcast([P, NQ // 2, PACK]), op=ALU.mult)
@@ -189,7 +195,7 @@ def tile_attend_gate_topk_kernel(tc, qT, k_words, k_scales, vT, vs, og, offs, ou
         nc.scalar.activation(out=gate[:], in_=th[:], func=ACT.Copy, bias=0.5, scale=0.5)
         r_sum = sb.tile([P, 1], F32, name="r_sum", tag="weights_then_reciprocal", align_bytes=64)
         nc.vector.reciprocal(out=r_sum[:], in_=l_sum[:])
-        for u, queue in enumerate((nc.scalar, nc.sync)):
+        for u in range(2):
             cols = slice(u * HALF, (u + 1) * HALF)
             y_ps = ps.tile([P, HALF], F32, name="y_ps%d" % u)
             nc.tensor.matmul_mx(out=y_ps[:], lhsT=w_codes[:].bitcast(FP8X4), lhsT_scale=w_sc[:],
@@ -197,4 +203,4 @@ def tile_attend_gate_topk_kernel(tc, qT, k_words, k_scales, vT, vs, og, offs, ou
             res = sb.tile([P, HALF], F32, name="res%d" % u)
             nc.vector.scalar_tensor_tensor(out=res[:], in0=y_ps[:], scalar=r_sum[:], in1=gate[:, cols],
                                            op0=ALU.mult, op1=ALU.mult)
-            queue.dma_start(out=out[0, :, cols], in_=res[:])
+            nc.sync.dma_start(out=out[0, :, cols], in_=res[:])

@@ -12,7 +12,7 @@ QUADS = 4
 STAGED = 96
 HALF = DV // 2
 SHARE = 288
-SPLIT = 448
+SPLIT = 384
 
 FLOPS = 2 * NQ * N * (D + DV)
 
@@ -26,6 +26,7 @@ FP8X4 = mybir.dt.float8_e4m3fn_x4
 FP4X4 = mybir.dt.float4_e2m1fn_x4
 ACT = mybir.ActivationFunctionType
 ALU = mybir.AluOpType
+AXIS = mybir.AxisListType
 
 
 def tile_attend_gate_topk_kernel(tc, qT, k_words, k_scales, vT, vs, og, offs, out):
@@ -146,29 +147,36 @@ def tile_attend_gate_topk_kernel(tc, qT, k_words, k_scales, vT, vs, og, offs, ou
                 nc.tensor.transpose(bank[:, j, :], word_pairs[j], ident[:])
             return bank[:].rearrange("s j c -> s c j")
 
-        def quantise_values(u, v_il, codes):
-            nc.vector.quantize_mx(out=codes[:].bitcast(FP8X4), scales=v_sc[:, u * HALF:(u + 1) * HALF],
-                                  in_=v_il[:].rearrange("s c j -> s (c j)").bitcast(BF16))
+        def quantise_values(u, v_il, codes, part):
+            nc.vector.quantize_mx(out=codes[:, part].bitcast(FP8X4),
+                                  scales=v_sc[:, u * HALF + part.start:u * HALF + part.stop],
+                                  in_=v_il[:, part, :].rearrange("s c j -> s (c j)").bitcast(BF16))
 
         words0 = v_g0[:].bitcast(F32)
         words1 = v_g1[:].rearrange("c j s e -> c (j s e)").bitcast(F32)
         turned0 = turn_values(0, [words0[:, j:N // 2:2] for j in range(2)])
 
-        p_sb = [sb.tile([P, 2, P], F32, name="p_sb%d" % u, tag="exps%d" % u, align_bytes=64) for u in range(2)]
-        l_half = [sb.tile([P, 1], F32, name="l_half%d" % u) for u in range(2)]
+        p_first = sb.tile([P, 2 * P + 2], F32, name="p_first", align_bytes=64)
+        p_last = sb.tile([P, 2, P], F32, name="p_last", tag="exps_then_codes", align_bytes=64)
         p_ps = ps.tile([P, PACK, NQ], F32, name="p_ps")
-        for u in range(2):
-            nc.scalar.activation(out=p_sb[u][:], in_=neg_s[:, 2 * u:2 * u + 2, :], func=ACT.Exp,
-                                 bias=neg_m[1][:], scale=-1.0 if u else minus_one[:], accum_out=l_half[u][:])
-            for j in range(2):
-                nc.tensor.transpose(p_ps[:, 2 * u + j, :], p_sb[u][:, j, :], ident[:])
+        nc.scalar.activation(out=p_first[:, 0:2 * P], in_=neg_s[:, 0:2, :].rearrange("q j s -> q (j s)"),
+                             func=ACT.Exp, bias=neg_m[1][:], scale=minus_one[:])
+        for j in range(2):
+            nc.tensor.transpose(p_ps[:, j, :], p_first[:, j * P:(j + 1) * P], ident[:])
+        for j in range(2):
+            nc.scalar.activation(out=p_last[:, j, :], in_=neg_s[:, 2 + j, :], func=ACT.Exp,
+                                 bias=neg_m[1][:], scale=-1.0, accum_out=p_first[:, 2 * P + j:2 * P + j + 1])
+            nc.tensor.transpose(p_ps[:, 2 + j, :], p_last[:, j, :], ident[:])
+        l_sum = sb.tile([P, 1], F32, name="l_sum")
+        nc.vector.tensor_reduce(out=l_sum[:], in_=p_first[:], axis=AXIS.X, op=ALU.add)
 
         v_il0 = sb.tile([P, HALF, 2], F32, name="v_il0", tag="sign_then_values", align_bytes=64)
         nc.scalar.copy(out=v_il0[:], in_=turned0)
         v_il1 = sb.tile([P, HALF, 2], F32, name="v_il1", align_bytes=64)
-        nc.scalar.copy(out=v_il1[:], in_=turn_values(1, [words1[:, j * P:(j + 1) * P] for j in range(2)]))
-        l_sum = sb.tile([P, 1], F32, name="l_sum")
-        nc.scalar.activation(out=l_sum[:], in_=l_half[0][:], func=ACT.Identity, bias=l_half[1][:], scale=1.0)
+        turned1 = turn_values(1, [words1[:, j * P:(j + 1) * P] for j in range(2)])
+        feature_halves = (slice(0, HALF // 2), slice(HALF // 2, HALF))
+        for part in feature_halves:
+            nc.scalar.copy(out=v_il1[:, part, :], in_=turned1[:, part, :])
 
         w_il = sb.tile([P, NQ, PACK], BF16, name="w_il", tag="weights_then_reciprocal", align_bytes=64)
         w_codes = sb.tile([P, NQ], U32, name="w_codes", align_bytes=64)
@@ -182,11 +190,12 @@ def tile_attend_gate_topk_kernel(tc, qT, k_words, k_scales, vT, vs, og, offs, ou
                                   in_=w_il[:, rows, :].rearrange("s q t -> s (q t)"))
 
         quantise_weights(query_halves[0])
-        v_codes0 = sb.tile([P, HALF], U32, name="v_codes0", tag="exps1", align_bytes=64)
-        quantise_values(0, v_il0, v_codes0)
+        v_codes0 = sb.tile([P, HALF], U32, name="v_codes0", tag="exps_then_codes", align_bytes=64)
+        quantise_values(0, v_il0, v_codes0, slice(0, HALF))
         quantise_weights(query_halves[1])
         v_codes1 = sb.tile([P, HALF], U32, name="v_codes1", tag="scales_then_codes", align_bytes=64)
-        quantise_values(1, v_il1, v_codes1)
+        for part in feature_halves:
+            quantise_values(1, v_il1, v_codes1, part)
         v_codes = (v_codes0, v_codes1)
 
         th = sb.tile([P, DV], F32, name="th")
@@ -195,12 +204,14 @@ def tile_attend_gate_topk_kernel(tc, qT, k_words, k_scales, vT, vs, og, offs, ou
         nc.scalar.activation(out=gate[:], in_=th[:], func=ACT.Copy, bias=0.5, scale=0.5)
         r_sum = sb.tile([P, 1], F32, name="r_sum", tag="weights_then_reciprocal", align_bytes=64)
         nc.vector.reciprocal(out=r_sum[:], in_=l_sum[:])
-        for u in range(2):
-            cols = slice(u * HALF, (u + 1) * HALF)
-            y_ps = ps.tile([P, HALF], F32, name="y_ps%d" % u)
-            nc.tensor.matmul_mx(out=y_ps[:], lhsT=w_codes[:].bitcast(FP8X4), lhsT_scale=w_sc[:],
-                                rhs=v_codes[u][:].bitcast(FP8X4), rhs_scale=v_sc[:, cols], start=True, stop=True)
+        for u, parts in enumerate(((slice(0, HALF),), feature_halves)):
             res = sb.tile([P, HALF], F32, name="res%d" % u)
-            nc.vector.scalar_tensor_tensor(out=res[:], in0=y_ps[:], scalar=r_sum[:], in1=gate[:, cols],
-                                           op0=ALU.mult, op1=ALU.mult)
-            nc.sync.dma_start(out=out[0, :, cols], in_=res[:])
+            for part in parts:
+                cols = slice(u * HALF + part.start, u * HALF + part.stop)
+                y_ps = ps.tile([P, part.stop - part.start], F32, name="y_ps%d" % cols.start)
+                nc.tensor.matmul_mx(out=y_ps[:], lhsT=w_codes[:].bitcast(FP8X4), lhsT_scale=w_sc[:],
+                                    rhs=v_codes[u][:, part].bitcast(FP8X4), rhs_scale=v_sc[:, cols],
+                                    start=True, stop=True)
+                nc.vector.scalar_tensor_tensor(out=res[:, part], in0=y_ps[:], scalar=r_sum[:], in1=gate[:, cols],
+                                               op0=ALU.mult, op1=ALU.mult)
+            nc.sync.dma_start(out=out[0, :, u * HALF:(u + 1) * HALF], in_=res[:])

@@ -156,19 +156,20 @@ def tile_attend_gate_topk_kernel(tc, qT, k_words, k_scales, vT, vs, og, offs, ou
         words1 = v_g1[:].rearrange("c j s e -> c (j s e)").bitcast(F32)
         turned0 = turn_values(0, [words0[:, j:N // 2:2] for j in range(2)])
 
-        p_first = sb.tile([P, 2 * P + 2], F32, name="p_first", align_bytes=64)
+        p_first = sb.tile([P, 2 * P], F32, name="p_first", align_bytes=64)
+        sums = sb.tile([P, 3], F32, name="sums")
         p_last = sb.tile([P, 2, P], F32, name="p_last", tag="exps_then_codes", align_bytes=64)
         p_ps = ps.tile([P, PACK, NQ], F32, name="p_ps")
-        nc.scalar.activation(out=p_first[:, 0:2 * P], in_=neg_s[:, 0:2, :].rearrange("q j s -> q (j s)"),
-                             func=ACT.Exp, bias=neg_m[1][:], scale=minus_one[:])
+        nc.scalar.activation(out=p_first[:], in_=neg_s[:, 0:2, :].rearrange("q j s -> q (j s)"),
+                             func=ACT.Exp, bias=neg_m[1][:], scale=minus_one[:], accum_out=sums[:, 0:1])
         for j in range(2):
             nc.tensor.transpose(p_ps[:, j, :], p_first[:, j * P:(j + 1) * P], ident[:])
         for j in range(2):
             nc.scalar.activation(out=p_last[:, j, :], in_=neg_s[:, 2 + j, :], func=ACT.Exp,
-                                 bias=neg_m[1][:], scale=-1.0, accum_out=p_first[:, 2 * P + j:2 * P + j + 1])
+                                 bias=neg_m[1][:], scale=-1.0, accum_out=sums[:, 1 + j:2 + j])
             nc.tensor.transpose(p_ps[:, 2 + j, :], p_last[:, j, :], ident[:])
         l_sum = sb.tile([P, 1], F32, name="l_sum")
-        nc.vector.tensor_reduce(out=l_sum[:], in_=p_first[:], axis=AXIS.X, op=ALU.add)
+        nc.vector.tensor_reduce(out=l_sum[:], in_=sums[:], axis=AXIS.X, op=ALU.add)
 
         v_il0 = sb.tile([P, HALF, 2], F32, name="v_il0", tag="sign_then_values", align_bytes=64)
         nc.scalar.copy(out=v_il0[:], in_=turned0)

from contextlib import ExitStack

import concourse.mybir as mybir
from concourse.masks import make_identity

T, N, D, DV, NQ = 1024, 512, 1024, 256, 128
P = 128
PACK = 4
PASSES = D // (P * PACK)
SCALE_ROWS = 4
QUADS = 4
STAGED = 96
HALF = DV // 2
SHARE = 288
SPLIT = 384

FLOPS = 2 * NQ * N * (D + DV)

F32 = mybir.dt.float32
BF16 = mybir.dt.bfloat16
I32 = mybir.dt.int32
U32 = mybir.dt.uint32
U16 = mybir.dt.uint16
U8 = mybir.dt.uint8
FP8X4 = mybir.dt.float8_e4m3fn_x4
FP4X4 = mybir.dt.float4_e2m1fn_x4
ACT = mybir.ActivationFunctionType
ALU = mybir.AluOpType
AXIS = mybir.AxisListType


def tile_attend_gate_topk_kernel(tc, qT, k_words, k_scales, vT, vs, og, offs, out):
    nc = tc.nc
    with ExitStack() as ctx:
        sb = ctx.enter_context(tc.tile_pool(name="sb", bufs=1))
        ps = ctx.enter_context(tc.psum_pool(name="ps", bufs=1))

        offsets = sb.tile([P, N // 16], U16, name="offsets")
        ks_pool = sb.tile([P, T], U8, name="ks_pool", tag="scale_rows_then_values", align_bytes=64)
        vs_pool = sb.tile([P, T], F32, name="vs_pool", tag="token_scales_then_gate", align_bytes=64)
        kw_pool = sb.tile([P, T], I32, name="kw_pool")
        planes = sb.tile([P, PASSES, N], U8, name="planes", align_bytes=64)
        scales_and_queries = sb.tile([P, N // 2 + PACK * NQ], F32, name="scales_and_queries", align_bytes=64)
        q_raw1 = sb.tile([P, PACK, NQ], F32, name="q_raw1", tag="queries1", align_bytes=64)
        q_raw = [scales_and_queries[:, N // 2:].rearrange("p (j q) -> p j q", j=PACK), q_raw1[:]]
        v_raw0 = sb.tile([P, T], F32, name="v_raw0", align_bytes=64)
        ident = sb.tile([P, P], F32, name="ident")

        ks_words = ks_pool[:].bitcast(I32)
        nc.sync.dma_start(offsets[:], offs)
        nc.scalar.dma_start(out=ks_words[STAGED:P, :], in_=k_scales.bitcast(I32).rearrange("o f w -> f o w"))
        nc.scalar.dma_start(out=vs_pool[P - 1:P, :], in_=vs[0:1, :])
        one = sb.tile([P, 1], F32, name="one")
        nc.vector.memset(one[:], 1.0)
        minus_one = sb.tile([P, 1], F32, name="minus_one", tag="sign_then_values", align_bytes=64)
        nc.scalar.activation(out=minus_one[:], in_=one[:], func=ACT.Copy, scale=-1.0)
        nc.vector.memset(ks_words[0:STAGED, :], 0)
        nc.vector.memset(vs_pool[0:P - 1, :], 0.0)
        nc.sync.dma_start(out=kw_pool[:], in_=k_words[0].rearrange("p t b -> p (t b)").bitcast(I32))
        q_rows = qT[0].rearrange("(o p j) q -> o p j q", o=PASSES, j=PACK)
        for o in range(PASSES):
            nc.sync.dma_start(out=q_raw[o], in_=q_rows[o])
        nc.sync.dma_start(out=v_raw0[:], in_=vT[0:HALF, :])
        plane_words = planes[:].rearrange("p o n -> p (o n)").bitcast(I32)
        nc.vector.memset(plane_words, 0)
        make_identity(nc, ident[:])

        ks_g = sb.tile([P, N], U8, name="ks_g", align_bytes=64)
        nc.vector.tensor_copy(out=ks_g[:], in_=ks_pool[:].indirect(offsets[:]))
        rows_a_quad = SCALE_ROWS * PASSES
        for quad in range(QUADS):
            lo = STAGED + quad * rows_a_quad
            nc.sync.dma_start(out=plane_words[32 * quad:32 * quad + SCALE_ROWS, :],
                              in_=ks_g[:].bitcast(I32)[lo:lo + rows_a_quad, :])
        v_raw1 = sb.tile([P, T], F32, name="v_raw1", tag="scale_rows_then_values", align_bytes=64)
        nc.sync.dma_start(out=v_raw1[:], in_=vT[HALF:DV, :])

        kw_g = [sb.tile([P, N // 2], U32, name="kw_g%d" % h, align_bytes=64) for h in range(2)]
        for h in range(2):
            nc.vector.tensor_copy(out=kw_g[h][:],
                                  in_=kw_pool[:].bitcast(U32).indirect(offsets[:, h * N // 32:(h + 1) * N // 32]))

        def word_halves(h):
            return kw_g[h][:].bitcast(U16).rearrange("p (n o) -> p o n", o=PASSES)

        first_keys = sb.tile([P, PASSES, N // 2], U16, name="first_keys", align_bytes=64)
        nc.vector.tensor_copy(out=first_keys[:], in_=word_halves(0))

        q_il = [sb.tile([P, NQ, PACK], BF16, name="q_il%d" % o, align_bytes=64) for o in range(PASSES)]
        q_codes = [sb.tile([P, NQ], U32, name="q_codes%d" % o, align_bytes=64) for o in range(PASSES)]
        q_sc = [sb.tile([P, NQ], U8, name="q_sc%d" % o, align_bytes=64) for o in range(PASSES)]

        def quantise_queries(o, rows):
            nc.scalar.activation(out=q_il[o][:, rows, :].rearrange("p (c i) j -> p c j i", i=PACK),
                                 in_=q_raw[o][:, :, rows].rearrange("p j (c i) -> p c j i", i=PACK), func=ACT.Copy)
            nc.vector.quantize_mx(out=q_codes[o][:, rows].bitcast(FP8X4), scales=q_sc[o][:, rows],
                                  in_=q_il[o][:, rows, :].rearrange("p q j -> p (q j)"))

        query_halves = (slice(0, NQ // 2), slice(NQ // 2, NQ))
        quantise_queries(0, slice(0, NQ))
        quantise_queries(1, query_halves[0])
        quantise_queries(1, query_halves[1])
        second_keys = sb.tile([P, PASSES, N // 2], U16, name="second_keys", tag="queries1", align_bytes=64)
        for o in range(PASSES):
            nc.vector.tensor_copy(out=second_keys[:, o, :], in_=word_halves(1)[:, o, :])
        k_op = (first_keys, second_keys)

        vs_g = scales_and_queries[:, 0:N]
        for h in range(2):
            nc.scalar.activation(out=vs_g[:, h * N // 2:(h + 1) * N // 2], func=ACT.Copy,
                                 in_=vs_pool[:].indirect(offsets[:, h * N // 32:(h + 1) * N // 32]))
        vs_col = sb.tile([P, PACK], F32, name="vs_col", tag="scales_then_codes", align_bytes=64)
        nc.sync.dma_start(out=vs_col[:], in_=vs_g[P - 1:P, :])
        gate_in = sb.tile([P, DV], F32, name="gate_in", tag="token_scales_then_gate", align_bytes=64)
        nc.sync.dma_start(out=gate_in[:], in_=og[0])

        neg_s = sb.tile([P, PACK, P], F32, name="neg_s")
        neg_m = [sb.tile([P, 1], F32, name="neg_m%d" % h) for h in range(2)]
        for h in range(2):
            scores = ps.tile([P, N // 2], F32, name="scores%d" % h, tag="bank%d" % h)
            for o in range(PASSES):
                nc.tensor.matmul_mx(out=scores[:], lhsT=q_codes[o][:].bitcast(FP8X4), lhsT_scale=q_sc[o][:],
                                    rhs=k_op[h][:, o, :].bitcast(FP4X4),
                                    rhs_scale=planes[:, o, h * N // 2:(h + 1) * N // 2],
                                    start=(o == 0), stop=(o == PASSES - 1))
            nc.vector.tensor_scalar(out=neg_s[:, :, h * P // 2:(h + 1) * P // 2],
                                    in0=scores[:].rearrange("q (s t) -> q t s", t=PACK),
                                    scalar1=-1.0, scalar2=neg_m[0][:] if h else None, op0=ALU.mult, op1=ALU.min,
                                    accum_out=neg_m[h][:])

        v_g0 = sb.tile([P, N], BF16, name="v_g0", align_bytes=64)
        nc.vector.tensor_copy(out=v_g0[:, 0:SHARE], in_=v_raw0[:].indirect(offsets[:, 0:SHARE // 16]))
        nc.scalar.activation(out=v_g0[:, SHARE:N], in_=v_raw0[:].indirect(offsets[:, SHARE // 16:N // 16]), func=ACT.Copy)
        v_g1 = sb.tile([P, 2, P, 2], BF16, name="v_g1", tag="queries1", align_bytes=64)
        nc.vector.tensor_copy(out=v_g1[:, :, 0:SPLIT // PACK, :].rearrange("c j s e -> c s j e"),
                              in_=v_raw1[:].indirect(offsets[:, 0:SPLIT // 16]))
        v_rest = sb.tile([P, N - SPLIT], BF16, name="v_rest", align_bytes=64)
        nc.scalar.activation(out=v_rest[:], in_=v_raw1[:].indirect(offsets[:, SPLIT // 16:N // 16]), func=ACT.Copy)
        nc.gpsimd.tensor_copy(
            out=v_g1[:].rearrange("c j s e -> c (j s e)").bitcast(I32).rearrange("c (j s) -> c j s", j=2)[:, :, SPLIT // PACK:P],
            in_=v_rest[:].bitcast(I32).rearrange("c (s j) -> c j s", j=2))
        v_sc = sb.tile([P, DV], U8, name="v_sc", align_bytes=64)

        def turn_values(u, word_pairs):
            bank = ps.tile([P, 2, P], F32, name="v_ps%d" % u, tag="bank0")
            for j in range(2):
                nc.tensor.transpose(bank[:, j, :], word_pairs[j], ident[:])
            return bank[:].rearrange("s j c -> s c j")

        def quantise_values(u, v_il, codes, part):
            nc.vector.quantize_mx(out=codes[:, part].bitcast(FP8X4),
                                  scales=v_sc[:, u * HALF + part.start:u * HALF + part.stop],
                                  in_=v_il[:, part, :].rearrange("s c j -> s (c j)").bitcast(BF16))

        words0 = v_g0[:].bitcast(F32)
        words1 = v_g1[:].rearrange("c j s e -> c (j s e)").bitcast(F32)
        turned0 = turn_values(0, [words0[:, j:N // 2:2] for j in range(2)])

        p_first = sb.tile([P, 2 * P], F32, name="p_first", align_bytes=64)
        sums = sb.tile([P, 3], F32, name="sums")
        p_last = sb.tile([P, 2, P], F32, name="p_last", tag="exps_then_codes", align_bytes=64)
        p_ps = ps.tile([P, PACK, NQ], F32, name="p_ps")
        nc.scalar.activation(out=p_first[:], in_=neg_s[:, 0:2, :].rearrange("q j s -> q (j s)"),
                             func=ACT.Exp, bias=neg_m[1][:], scale=minus_one[:], accum_out=sums[:, 0:1])
        for j in range(2):
            nc.tensor.transpose(p_ps[:, j, :], p_first[:, j * P:(j + 1) * P], ident[:])
        for j in range(2):
            nc.scalar.activation(out=p_last[:, j, :], in_=neg_s[:, 2 + j, :], func=ACT.Exp,
                                 bias=neg_m[1][:], scale=-1.0, accum_out=sums[:, 1 + j:2 + j])
            nc.tensor.transpose(p_ps[:, 2 + j, :], p_last[:, j, :], ident[:])
        l_sum = sb.tile([P, 1], F32, name="l_sum")
        nc.vector.tensor_reduce(out=l_sum[:], in_=sums[:], axis=AXIS.X, op=ALU.add)

        v_il0 = sb.tile([P, HALF, 2], F32, name="v_il0", tag="sign_then_values", align_bytes=64)
        nc.scalar.copy(out=v_il0[:], in_=turned0)
        v_il1 = sb.tile([P, HALF, 2], F32, name="v_il1", align_bytes=64)
        turned1 = turn_values(1, [words1[:, j * P:(j + 1) * P] for j in range(2)])
        feature_halves = (slice(0, HALF // 2), slice(HALF // 2, HALF))
        for part in feature_halves:
            nc.scalar.copy(out=v_il1[:, part, :], in_=turned1[:, part, :])

        w_il = sb.tile([P, NQ, PACK], BF16, name="w_il", tag="weights_then_reciprocal", align_bytes=64)
        w_codes = sb.tile([P, NQ], U32, name="w_codes", align_bytes=64)
        w_sc = sb.tile([P, NQ], U8, name="w_sc", align_bytes=64)
        for rows in query_halves:
            nc.vector.tensor_tensor(out=w_il[:, rows, :], in0=p_ps[:, :, rows].rearrange("s t q -> s q t"),
                                    in1=vs_col[:].unsqueeze(1).to_broadcast([P, NQ // 2, PACK]), op=ALU.mult)

        def quantise_weights(rows):
            nc.vector.quantize_mx(out=w_codes[:, rows].bitcast(FP8X4), scales=w_sc[:, rows],
                                  in_=w_il[:, rows, :].rearrange("s q t -> s (q t)"))

        quantise_weights(query_halves[0])
        v_codes0 = sb.tile([P, HALF], U32, name="v_codes0", tag="exps_then_codes", align_bytes=64)
        quantise_values(0, v_il0, v_codes0, slice(0, HALF))
        quantise_weights(query_halves[1])
        v_codes1 = sb.tile([P, HALF], U32, name="v_codes1", tag="scales_then_codes", align_bytes=64)
        for part in feature_halves:
            quantise_values(1, v_il1, v_codes1, part)
        v_codes = (v_codes0, v_codes1)

        th = sb.tile([P, DV], F32, name="th")
        nc.scalar.activation(out=th[:], in_=gate_in[:], func=ACT.Tanh, scale=0.5)
        gate = sb.tile([P, DV], F32, name="gate")
        nc.scalar.activation(out=gate[:], in_=th[:], func=ACT.Copy, bias=0.5, scale=0.5)
        r_sum = sb.tile([P, 1], F32, name="r_sum", tag="weights_then_reciprocal", align_bytes=64)
        nc.vector.reciprocal(out=r_sum[:], in_=l_sum[:])
        for u, parts in enumerate(((slice(0, HALF),), feature_halves)):
            res = sb.tile([P, HALF], F32, name="res%d" % u)
            for part in parts:
                cols = slice(u * HALF + part.start, u * HALF + part.stop)
                y_ps = ps.tile([P, part.stop - part.start], F32, name="y_ps%d" % cols.start)
                nc.tensor.matmul_mx(out=y_ps[:], lhsT=w_codes[:].bitcast(FP8X4), lhsT_scale=w_sc[:],
                                    rhs=v_codes[u][:, part].bitcast(FP8X4), rhs_scale=v_sc[:, cols],
                                    start=True, stop=True)
                nc.vector.scalar_tensor_tensor(out=res[:, part], in0=y_ps[:], scalar=r_sum[:], in1=gate[:, cols],
                                               op0=ALU.mult, op1=ALU.mult)
            nc.sync.dma_start(out=out[0, :, u * HALF:(u + 1) * HALF], in_=res[:])
